import numpy as np
import ml_dtypes


def mxq(x, axis, fmt="e4m3"):
    dtype, down = {"e4m3": (ml_dtypes.float8_e4m3fn, 7), "e5m2": (ml_dtypes.float8_e5m2, 14)}[fmt]
    v = np.moveaxis(np.asarray(x, np.float32).astype(ml_dtypes.bfloat16).astype(np.float64), axis, -1)
    blocks = v.reshape(v.shape[:-1] + (-1, 32))
    amax = np.abs(blocks).max(-1, keepdims=True)
    byte = np.maximum(np.where(amax > 0, np.frexp(amax)[1] - 1 + 127, 0) - down, 1)
    scale = np.exp2(byte - 127.0)
    codes = (blocks / scale).astype(np.float32).astype(dtype).astype(np.float64)
    return np.moveaxis((codes * scale).reshape(v.shape), -1, axis)


WIDE = False


def mx_kscale(k):
    if not WIDE:
        return np.ones(k)
    levels = np.array([10, -10, 5, -5, 0])
    if k % 512:
        return np.exp2(np.random.permutation(np.resize(levels, k // 32))).repeat(32)
    a = np.empty((k // 512, 16))
    for p in range(k // 512):
        a[p, :8] = np.random.permutation(np.resize(levels, 8))
        for g in range(8):
            far = levels[np.abs(levels - a[p, g]) >= 10]
            a[p, g + 8] = far[np.random.randint(len(far))]
    return np.exp2(a.ravel()).repeat(32)


def f64(x):
    return np.asarray(x).astype(np.float64)


def striped(idx):
    return np.tile(np.asarray(idx).reshape(-1, 16).T, (8, 1)).astype(np.uint16)


def unstriped(offs):
    return offs[:16].T.reshape(-1).astype(np.int64)


B, N, T, D, NQ = 2, 512, 2048, 512, 128


def setup_inputs():
    n = np.random.standard_normal
    jdx = np.random.permutation(1024)[:B * NQ]
    pages = np.random.permutation(T // 64)[:B * N // 64]
    idx = (pages[:, None] * 64 + np.arange(64)[None, :]).reshape(-1)
    s = mx_kscale(D)[:, None]
    return {
        "qT": (n((D, 1024)) * s * (1.00 / np.sqrt(D))).astype(np.float32),
        "kT": (n((D, T)) / s).astype(np.float32),
        "kb": np.tile(n(2048), (128, 1)).astype(np.float32),
        "offq": striped(jdx),
        "offs": striped(idx),
    }


def reference(qT, kT, kb, offq, offs):
    jdx = unstriped(offq)
    idx = unstriped(offs)
    pick = lambda x, which: x[:, which].reshape(x.shape[0], B, -1).transpose(1, 0, 2)
    qg = mxq(pick(f64(qT), jdx), 1, "e4m3")
    kg = mxq(pick(f64(kT), idx), 1, "e4m3")
    qq = qg
    a = qq.transpose(0, 2, 1) @ kg
    z = a + pick(f64(kb), idx)[:, :1, :]
    m = np.max(z, axis=-1, keepdims=True)
    e = np.exp(z - m)
    y = e / np.sum(e, axis=-1, keepdims=True)
    return y

@@ -1,0 +1,155 @@
+from contextlib import ExitStack
+
+import concourse.mybir as mybir
+from concourse.masks import make_identity
+
+B, N, T, D, NQ, TQ = 2, 512, 2048, 512, 128, 1024
+FLOPS = 2 * B * NQ * N * D
+BYTES = 4 * (D * TQ + D * T + T + B * NQ * N) + 2 * 128 * (16 + 64)
+
+F32 = mybir.dt.float32
+BF16 = mybir.dt.bfloat16
+U32 = mybir.dt.uint32
+U16 = mybir.dt.uint16
+U8 = mybir.dt.uint8
+FP8X4 = mybir.dt.float8_e4m3fn_x4
+ALU = mybir.AluOpType
+ACT = mybir.ActivationFunctionType
+AX = mybir.AxisListType
+
+P = 128
+PACK = 4
+PAGE = 64
+HALF = PAGE // 2
+K_CHUNKS = (512, 512, 512, 256, 256)
+Q_CHUNKS = ((512, 512), (512, 256, 256))
+KB_COLS = T // P
+BANK = 512
+
+
+def tile_attend_bothw_f_kernel(tc, qT, kT, kb, offq, offs, out):
+    nc = tc.nc
+    with ExitStack() as ctx:
+        keep = ctx.enter_context(tc.tile_pool(name="keep", bufs=1))
+        psum = ctx.enter_context(tc.psum_pool(name="psum", bufs=1))
+
+        key_list = keep.tile([P, B * N // 16], U16, name="key_list")
+        query_list = keep.tile([P, B * NQ // 16], U16, name="query_list")
+        bias_row = keep.tile([P, KB_COLS], F32, name="bias_row")
+        k_rows = kT.rearrange("(p t) c -> p t c", t=PACK)
+        q_rows = qT.rearrange("(p t) c -> p t c", t=PACK)
+
+        nc.sync.dma_start(bias_row[:], kb[0:1, :].rearrange("o (p j) -> (o p) j", j=KB_COLS))
+        k_raw = []
+        c0 = 0
+        for i, width in enumerate(K_CHUNKS):
+            raw = keep.tile([P, PACK, width], F32, name=f"k_raw{i}")
+            nc.sync.dma_start(raw[:], k_rows[:, :, c0 : c0 + width])
+            k_raw.append((raw, c0, width))
+            c0 = c0 + width
+            if i == 0:
+                nc.sync.dma_start(key_list[:], offs)
+                nc.sync.dma_start(query_list[:], offq)
+        q_raw = []
+        for u, widths in enumerate(Q_CHUNKS):
+            c0 = 0
+            for i, width in enumerate(widths):
+                raw = keep.tile([P, 2, width], F32, name=f"q_raw{u}_{i}")
+                nc.sync.dma_start(raw[:], q_rows[:, 2 * u : 2 * u + 2, c0 : c0 + width])
+                q_raw.append((raw, u, c0, width))
+                c0 = c0 + width
+
+        ident = keep.tile([P, P], F32, name="ident")
+        make_identity(nc, ident[:])
+        bias_pool = keep.tile([P, T], F32, name="bias_pool")
+        bias_view = bias_pool[:].rearrange("m (p g i) -> m g p i", g=KB_COLS // 4, i=4)
+        for g in range(KB_COLS // 4):
+            spread = psum.tile([P, 4, P], F32, name=f"spread{g}")
+            for i in range(4):
+                j = 4 * g + i
+                nc.tensor.transpose(spread[:, i, :], bias_row[:, j : j + 1].to_broadcast([P, P]), ident[:])
+            if g % 2 == 0:
+                nc.vector.tensor_copy(bias_view[:, g], spread[:].rearrange("m i p -> m p i"))
+            else:
+                nc.scalar.copy(bias_view[:, g], spread[:].rearrange("m i p -> m p i"))
+        bias = keep.tile([P, B * N], F32, name="bias")
+        nc.vector.tensor_copy(bias[:], bias_pool[:].indirect(key_list[:]))
+
+        k_pool = [keep.tile([P, T * 2], BF16, name=f"k_pool{h}") for h in range(2)]
+        for raw, c0, width in k_raw:
+            src = raw[:].rearrange("p t (g h r) -> p h g r t", h=2, r=HALF)
+            for h in range(2):
+                dst = k_pool[h][:, 2 * c0 : 2 * (c0 + width)].rearrange("p (g r t) -> p g r t", r=HALF, t=PACK)
+                if h == 0:
+                    nc.vector.tensor_copy(dst, src[:, h])
+                else:
+                    nc.scalar.copy(dst, src[:, h])
+
+        k_codes = [keep.tile([P, N], U32, name=f"k_codes{b}", align_bytes=64) for b in range(B)]
+        k_scales = [keep.tile([P, N], U8, name=f"k_scales{b}", align_bytes=64) for b in range(B)]
+        k_listed = []
+        for h in range(2):
+            listed = keep.tile([P, B * N * 2], BF16, name=f"k_listed{h}", align_bytes=64)
+            nc.vector.tensor_copy(listed[:].bitcast(U32), k_pool[h][:].bitcast(U32).indirect(key_list[:]))
+            k_listed.append(listed)
+        for h in range(2):
+            for b in range(B):
+                cols = slice(h * N // 2, (h + 1) * N // 2)
+                nc.vector.quantize_mx(
+                    out=k_codes[b][:, cols].bitcast(FP8X4),
+                    scales=k_scales[b][:, cols],
+                    in_=k_listed[h][:, b * N * 2 : (b + 1) * N * 2],
+                )
+
+        q_pool = [keep.tile([P, TQ * 2], BF16, name=f"q_pool{u}") for u in range(2)]
+        for raw, u, c0, width in q_raw:
+            dst = q_pool[u][:, 2 * c0 : 2 * (c0 + width)].rearrange("p (c t) -> p c t", t=2)
+            nc.scalar.copy(dst, raw[:].rearrange("p t c -> p c t"))
+        q_listed = [keep.tile([P, NQ * PACK], BF16, name=f"q_listed{b}", align_bytes=64) for b in range(B)]
+        for u in range(2):
+            for b in range(B):
+                dst = q_listed[b][:].bitcast(U32).rearrange("p (c u) -> p u c", u=2)
+                cols = slice(b * NQ // 16, (b + 1) * NQ // 16)
+                nc.vector.tensor_copy(dst[:, u], q_pool[u][:].bitcast(U32).indirect(query_list[:, cols]))
+
+        scores = []
+        for b in range(B):
+            q_codes = keep.tile([P, NQ], U32, name=f"q_codes{b}", align_bytes=64)
+            q_scales = keep.tile([P, NQ], U8, name=f"q_scales{b}", align_bytes=64)
+            nc.vector.quantize_mx(out=q_codes[:].bitcast(FP8X4), scales=q_scales[:], in_=q_listed[b][:])
+            acc = psum.tile([P, N], F32, name=f"scores{b}")
+            nc.tensor.matmul_mx(
+                out=acc[:],
+                lhsT=q_codes[:].bitcast(FP8X4),
+                lhsT_scale=q_scales[:],
+                rhs=k_codes[b][:].bitcast(FP8X4),
+                rhs_scale=k_scales[b][:],
+                start=True,
+                stop=True,
+            )
+            scores.append(acc)
+
+        z = []
+        for b in range(B):
+            zb = keep.tile([P, N], F32, name=f"z{b}")
+            nc.vector.tensor_tensor(
+                zb[:].rearrange("q (j h r) -> q j h r", h=2, r=HALF),
+                scores[b][:].rearrange("q (h j r) -> q j h r", h=2, r=HALF),
+                bias[:, b * N : (b + 1) * N].rearrange("q (j h r) -> q j h r", h=2, r=HALF),
+                ALU.add,
+            )
+            z.append(zb)
+        neg_max = []
+        for b in range(B):
+            nm = keep.tile([P, 1], F32, name=f"neg_max{b}")
+            nc.vector.tensor_reduce(nm[:], z[b][:], AX.X, ALU.max, negate=True)
+            neg_max.append(nm)
+        for b in range(B):
+            e = keep.tile([P, N], F32, name=f"e{b}")
+            total = keep.tile([P, 1], F32, name=f"total{b}")
+            nc.scalar.activation(e[:], z[b][:], ACT.Exp, bias=neg_max[b][:], scale=1.0, accum_out=total[:])
+            inverse = keep.tile([P, 1], F32, name=f"inverse{b}")
+            nc.vector.reciprocal(inverse[:], total[:])
+            y = keep.tile([P, N], F32, name=f"y{b}")
+            nc.vector.tensor_scalar(y[:], e[:], inverse[:], None, ALU.mult)
+            nc.sync.dma_start(out[b], y[:])

@@ -21,8 +21,7 @@ P = 128
 PACK = 4
 PAGE = 64
 HALF = PAGE // 2
-K_CHUNKS = (512, 512, 512, 256, 256)
-Q_CHUNKS = ((512, 512), (512, 256, 256))
+K_CHUNKS = ((0, 0, 1024), (0, 1024, 1024), (1, 0, 1024), (1, 1024, 512), (1, 1536, 512))
 KB_COLS = T // P
 BANK = 512
 
@@ -40,50 +39,41 @@ def tile_attend_bothw_f_kernel(tc, qT, kT, kb, offq, offs, out):
         q_rows = qT.rearrange("(p t) c -> p t c", t=PACK)
 
         nc.sync.dma_start(bias_row[:], kb[0:1, :].rearrange("o (p j) -> (o p) j", j=KB_COLS))
+        nc.sync.dma_start(key_list[:], offs)
         k_raw = []
-        c0 = 0
-        for i, width in enumerate(K_CHUNKS):
-            raw = keep.tile([P, PACK, width], F32, name=f"k_raw{i}")
-            nc.sync.dma_start(raw[:], k_rows[:, :, c0 : c0 + width])
-            k_raw.append((raw, c0, width))
-            c0 = c0 + width
+        for i, (u, c0, width) in enumerate(K_CHUNKS):
+            raw = keep.tile([P, 2, width], F32, name=f"k_raw{i}")
+            nc.sync.dma_start(raw[:], k_rows[:, 2 * u : 2 * u + 2, c0 : c0 + width])
+            k_raw.append(raw)
             if i == 0:
-                nc.sync.dma_start(key_list[:], offs)
                 nc.sync.dma_start(query_list[:], offq)
         q_raw = []
-        for u, widths in enumerate(Q_CHUNKS):
-            c0 = 0
-            for i, width in enumerate(widths):
-                raw = keep.tile([P, 2, width], F32, name=f"q_raw{u}_{i}")
-                nc.sync.dma_start(raw[:], q_rows[:, 2 * u : 2 * u + 2, c0 : c0 + width])
-                q_raw.append((raw, u, c0, width))
-                c0 = c0 + width
+        for t in range(PACK):
+            raw = keep.tile([P, TQ], F32, name=f"q_raw{t}")
+            nc.sync.dma_start(raw[:], q_rows[:, t, :])
+            q_raw.append(raw)
 
-        ident = keep.tile([P, P], F32, name="ident")
+        ident = keep.tile([P, P], F32, name="ident", tag="after_spread")
         make_identity(nc, ident[:])
-        bias_pool = keep.tile([P, T], F32, name="bias_pool")
+        bias_pool = keep.tile([P, T], F32, name="bias_pool", tag="after_bias")
         bias_view = bias_pool[:].rearrange("m (p g i) -> m g p i", g=KB_COLS // 4, i=4)
         for g in range(KB_COLS // 4):
             spread = psum.tile([P, 4, P], F32, name=f"spread{g}")
             for i in range(4):
                 j = 4 * g + i
                 nc.tensor.transpose(spread[:, i, :], bias_row[:, j : j + 1].to_broadcast([P, P]), ident[:])
-            if g % 2 == 0:
-                nc.vector.tensor_copy(bias_view[:, g], spread[:].rearrange("m i p -> m p i"))
-            else:
-                nc.scalar.copy(bias_view[:, g], spread[:].rearrange("m i p -> m p i"))
+            nc.scalar.copy(bias_view[:, g], spread[:].rearrange("m i p -> m p i"))
+
         bias = keep.tile([P, B * N], F32, name="bias")
         nc.vector.tensor_copy(bias[:], bias_pool[:].indirect(key_list[:]))
 
-        k_pool = [keep.tile([P, T * 2], BF16, name=f"k_pool{h}") for h in range(2)]
-        for raw, c0, width in k_raw:
-            src = raw[:].rearrange("p t (g h r) -> p h g r t", h=2, r=HALF)
+        k_pool = [keep.tile([P, T * 2], BF16, name=f"k_pool{h}", tag=("after_bias", "after_spread")[h]) for h in range(2)]
+        for i, (u, c0, width) in enumerate(K_CHUNKS):
+            src = k_raw[i][:].rearrange("p t (g h r) -> p h g r t", h=2, r=HALF)
             for h in range(2):
-                dst = k_pool[h][:, 2 * c0 : 2 * (c0 + width)].rearrange("p (g r t) -> p g r t", r=HALF, t=PACK)
-                if h == 0:
-                    nc.vector.tensor_copy(dst, src[:, h])
-                else:
-                    nc.scalar.copy(dst, src[:, h])
+                dst = k_pool[h][:, 2 * c0 : 2 * (c0 + width)].rearrange("p (g r u t) -> p u g r t", r=HALF, u=2, t=2)
+                copy = nc.vector.tensor_copy if h == 0 or i == 0 else nc.scalar.copy
+                copy(dst[:, u], src[:, h])
 
         k_codes = [keep.tile([P, N], U32, name=f"k_codes{b}", align_bytes=64) for b in range(B)]
         k_scales = [keep.tile([P, N], U8, name=f"k_scales{b}", align_bytes=64) for b in range(B)]
@@ -101,16 +91,18 @@ def tile_attend_bothw_f_kernel(tc, qT, kT, kb, offq, offs, out):
                     in_=k_listed[h][:, b * N * 2 : (b + 1) * N * 2],
                 )
 
-        q_pool = [keep.tile([P, TQ * 2], BF16, name=f"q_pool{u}") for u in range(2)]
-        for raw, u, c0, width in q_raw:
-            dst = q_pool[u][:, 2 * c0 : 2 * (c0 + width)].rearrange("p (c t) -> p c t", t=2)
-            nc.scalar.copy(dst, raw[:].rearrange("p t c -> p c t"))
         q_listed = [keep.tile([P, NQ * PACK], BF16, name=f"q_listed{b}", align_bytes=64) for b in range(B)]
-        for u in range(2):
+        for t in range(PACK):
+            if t < 2:
+                q_pool = keep.tile([P, TQ], BF16, name=f"q_pool{t}")
+                nc.scalar.copy(q_pool[:], q_raw[t][:])
             for b in range(B):
-                dst = q_listed[b][:].bitcast(U32).rearrange("p (c u) -> p u c", u=2)
-                cols = slice(b * NQ // 16, (b + 1) * NQ // 16)
-                nc.vector.tensor_copy(dst[:, u], q_pool[u][:].bitcast(U32).indirect(query_list[:, cols]))
+                dst = q_listed[b][:].rearrange("p (c t) -> p t c", t=PACK)[:, t]
+                listed = query_list[:, b * NQ // 16 : (b + 1) * NQ // 16]
+                if t < 2:
+                    nc.scalar.activation(dst, q_pool[:].indirect(listed), ACT.Copy)
+                else:
+                    nc.vector.tensor_copy(dst, q_raw[t][:].indirect(listed))
 
         scores = []
         for b in range(B):

@@ -9,6 +9,7 @@ BYTES = 4 * (D * TQ + D * T + T + B * NQ * N) + 2 * 128 * (16 + 64)
 
 F32 = mybir.dt.float32
 BF16 = mybir.dt.bfloat16
+I32 = mybir.dt.int32
 U32 = mybir.dt.uint32
 U16 = mybir.dt.uint16
 U8 = mybir.dt.uint8
@@ -19,17 +20,16 @@ AX = mybir.AxisListType
 
 P = 128
 PACK = 4
-PAGE = 64
-HALF = PAGE // 2
-K_CHUNKS = ((0, 0, 1024), (0, 1024, 1024), (1, 0, 1024), (1, 1024, 512), (1, 1536, 512))
 KB_COLS = T // P
-BANK = 512
+WINDOW_BYTES = 4 * T
+LISTED_BYTES = 2 * N * PACK
 
 
 def tile_attend_bothw_f_kernel(tc, qT, kT, kb, offq, offs, out):
     nc = tc.nc
     with ExitStack() as ctx:
         keep = ctx.enter_context(tc.tile_pool(name="keep", bufs=1))
+        placed = ctx.enter_context(tc.tile_pool(name="placed", bufs=1))
         psum = ctx.enter_context(tc.psum_pool(name="psum", bufs=1))
 
         key_list = keep.tile([P, B * N // 16], U16, name="key_list")
@@ -39,13 +39,14 @@ def tile_attend_bothw_f_kernel(tc, qT, kT, kb, offq, offs, out):
         q_rows = qT.rearrange("(p t) c -> p t c", t=PACK)
 
         nc.sync.dma_start(bias_row[:], kb[0:1, :].rearrange("o (p j) -> (o p) j", j=KB_COLS))
-        nc.sync.dma_start(key_list[:], offs)
         k_raw = []
-        for i, (u, c0, width) in enumerate(K_CHUNKS):
-            raw = keep.tile([P, 2, width], F32, name=f"k_raw{i}")
-            nc.sync.dma_start(raw[:], k_rows[:, 2 * u : 2 * u + 2, c0 : c0 + width])
+        for t in range(PACK):
+            raw = keep.tile([P, T], F32, name=f"k_raw{t}")
+            nc.sync.dma_start(raw[:], k_rows[:, t, :])
             k_raw.append(raw)
-            if i == 0:
+            if t == 0:
+                nc.sync.dma_start(key_list[:], offs)
+            if t == 2:
                 nc.sync.dma_start(query_list[:], offq)
         q_raw = []
         for t in range(PACK):
@@ -53,9 +54,9 @@ def tile_attend_bothw_f_kernel(tc, qT, kT, kb, offq, offs, out):
             nc.sync.dma_start(raw[:], q_rows[:, t, :])
             q_raw.append(raw)
 
-        ident = keep.tile([P, P], F32, name="ident", tag="after_spread")
+        ident = keep.tile([P, P], F32, name="ident")
         make_identity(nc, ident[:])
-        bias_pool = keep.tile([P, T], F32, name="bias_pool", tag="after_bias")
+        bias_pool = placed.tile([P, T], F32, name="bias_pool", offset=0)
         bias_view = bias_pool[:].rearrange("m (p g i) -> m g p i", g=KB_COLS // 4, i=4)
         for g in range(KB_COLS // 4):
             spread = psum.tile([P, 4, P], F32, name=f"spread{g}")
@@ -64,32 +65,30 @@ def tile_attend_bothw_f_kernel(tc, qT, kT, kb, offq, offs, out):
                 nc.tensor.transpose(spread[:, i, :], bias_row[:, j : j + 1].to_broadcast([P, P]), ident[:])
             nc.scalar.copy(bias_view[:, g], spread[:].rearrange("m i p -> m p i"))
 
+        k_low = keep.tile([P, 2 * B * N], BF16, name="k_low")
+        nc.vector.tensor_copy(k_low[:, 0 : B * N], k_raw[0][:].indirect(key_list[:]))
         bias = keep.tile([P, B * N], F32, name="bias")
         nc.vector.tensor_copy(bias[:], bias_pool[:].indirect(key_list[:]))
+        nc.vector.tensor_copy(k_low[:, B * N : 2 * B * N], k_raw[1][:].indirect(key_list[:]))
 
-        k_pool = [keep.tile([P, T * 2], BF16, name=f"k_pool{h}", tag=("after_bias", "after_spread")[h]) for h in range(2)]
-        for i, (u, c0, width) in enumerate(K_CHUNKS):
-            src = k_raw[i][:].rearrange("p t (g h r) -> p h g r t", h=2, r=HALF)
-            for h in range(2):
-                dst = k_pool[h][:, 2 * c0 : 2 * (c0 + width)].rearrange("p (g r u t) -> p u g r t", r=HALF, u=2, t=2)
-                copy = nc.vector.tensor_copy if h == 0 or i == 0 else nc.scalar.copy
-                copy(dst[:, u], src[:, h])
-
+        k_listed = [
+            placed.tile([P, N * PACK], BF16, name=f"k_listed{b}", align_bytes=64, offset=b * LISTED_BYTES)
+            for b in range(B)
+        ]
+        low_pairs = k_low[:].rearrange("p (t c) -> p c t", t=2)
+        for b in range(B):
+            words = k_listed[b][:].rearrange("p (c t) -> p c t", t=PACK)
+            nc.scalar.copy(words[:, :, 0:2], low_pairs[:, b * N : (b + 1) * N, :])
+        for t in range(2, PACK):
+            for b in range(B):
+                nc.vector.tensor_copy(
+                    k_listed[b][:].rearrange("p (c t) -> p t c", t=PACK)[:, t],
+                    k_raw[t][:].indirect(key_list[:, b * N // 16 : (b + 1) * N // 16]),
+                )
         k_codes = [keep.tile([P, N], U32, name=f"k_codes{b}", align_bytes=64) for b in range(B)]
         k_scales = [keep.tile([P, N], U8, name=f"k_scales{b}", align_bytes=64) for b in range(B)]
-        k_listed = []
-        for h in range(2):
-            listed = keep.tile([P, B * N * 2], BF16, name=f"k_listed{h}", align_bytes=64)
-            nc.vector.tensor_copy(listed[:].bitcast(U32), k_pool[h][:].bitcast(U32).indirect(key_list[:]))
-            k_listed.append(listed)
-        for h in range(2):
-            for b in range(B):
-                cols = slice(h * N // 2, (h + 1) * N // 2)
-                nc.vector.quantize_mx(
-                    out=k_codes[b][:, cols].bitcast(FP8X4),
-                    scales=k_scales[b][:, cols],
-                    in_=k_listed[h][:, b * N * 2 : (b + 1) * N * 2],
-                )
+        for b in range(B):
+            nc.vector.quantize_mx(out=k_codes[b][:].bitcast(FP8X4), scales=k_scales[b][:], in_=k_listed[b][:])
 
         q_listed = [keep.tile([P, NQ * PACK], BF16, name=f"q_listed{b}", align_bytes=64) for b in range(B)]
         for t in range(PACK):
@@ -124,12 +123,7 @@ def tile_attend_bothw_f_kernel(tc, qT, kT, kb, offq, offs, out):
         z = []
         for b in range(B):
             zb = keep.tile([P, N], F32, name=f"z{b}")
-            nc.vector.tensor_tensor(
-                zb[:].rearrange("q (j h r) -> q j h r", h=2, r=HALF),
-                scores[b][:].rearrange("q (h j r) -> q j h r", h=2, r=HALF),
-                bias[:, b * N : (b + 1) * N].rearrange("q (j h r) -> q j h r", h=2, r=HALF),
-                ALU.add,
-            )
+            nc.vector.tensor_tensor(zb[:], scores[b][:], bias[:, b * N : (b + 1) * N], ALU.add)
             z.append(zb)
         neg_max = []
         for b in range(B):

@@ -23,6 +23,7 @@ PACK = 4
 KB_COLS = T // P
 WINDOW_BYTES = 4 * T
 LISTED_BYTES = 2 * N * PACK
+LISTED_AT = WINDOW_BYTES + 2 * NQ * PACK
 
 
 def tile_attend_bothw_f_kernel(tc, qT, kT, kb, offq, offs, out):
@@ -54,7 +55,7 @@ def tile_attend_bothw_f_kernel(tc, qT, kT, kb, offq, offs, out):
             nc.sync.dma_start(raw[:], q_rows[:, t, :])
             q_raw.append(raw)
 
-        ident = keep.tile([P, P], F32, name="ident")
+        ident = placed.tile([P, P], F32, name="ident", offset=LISTED_AT + LISTED_BYTES - 2 * P)
         make_identity(nc, ident[:])
         bias_pool = placed.tile([P, T], F32, name="bias_pool", offset=0)
         bias_view = bias_pool[:].rearrange("m (p g i) -> m g p i", g=KB_COLS // 4, i=4)
@@ -71,26 +72,37 @@ def tile_attend_bothw_f_kernel(tc, qT, kT, kb, offq, offs, out):
         nc.vector.tensor_copy(bias[:], bias_pool[:].indirect(key_list[:]))
         nc.vector.tensor_copy(k_low[:, B * N : 2 * B * N], k_raw[1][:].indirect(key_list[:]))
 
+        k_high = placed.tile([P, 2 * B * N], BF16, name="k_high", offset=0)
+        nc.vector.tensor_copy(k_high[:, 0 : B * N], k_raw[2][:].indirect(key_list[:]))
+        for b in range(B):
+            nc.vector.tensor_copy(
+                k_high[:, (B + b) * N : (B + b + 1) * N],
+                k_raw[3][:].indirect(key_list[:, b * N // 16 : (b + 1) * N // 16]),
+            )
         k_listed = [
-            placed.tile([P, N * PACK], BF16, name=f"k_listed{b}", align_bytes=64, offset=b * LISTED_BYTES)
+            placed.tile([P, N * PACK], BF16, name=f"k_listed{b}", align_bytes=64, offset=LISTED_AT + b * LISTED_BYTES)
             for b in range(B)
         ]
-        low_pairs = k_low[:].rearrange("p (t c) -> p c t", t=2)
-        for b in range(B):
-            words = k_listed[b][:].rearrange("p (c t) -> p c t", t=PACK)
-            nc.scalar.copy(words[:, :, 0:2], low_pairs[:, b * N : (b + 1) * N, :])
-        for t in range(2, PACK):
+        for u, (planes, copy) in enumerate(((k_low, nc.scalar.copy), (k_high, nc.vector.tensor_copy))):
+            pairs = planes[:].rearrange("p (t c) -> p c t", t=2)
             for b in range(B):
-                nc.vector.tensor_copy(
-                    k_listed[b][:].rearrange("p (c t) -> p t c", t=PACK)[:, t],
-                    k_raw[t][:].indirect(key_list[:, b * N // 16 : (b + 1) * N // 16]),
-                )
+                words = k_listed[b][:].rearrange("p (c t) -> p c t", t=PACK)
+                copy(words[:, :, 2 * u : 2 * u + 2], pairs[:, b * N : (b + 1) * N, :])
         k_codes = [keep.tile([P, N], U32, name=f"k_codes{b}", align_bytes=64) for b in range(B)]
-        k_scales = [keep.tile([P, N], U8, name=f"k_scales{b}", align_bytes=64) for b in range(B)]
-        for b in range(B):
+        k_scales = [
+            keep.tile([P, N], U8, name="k_scales0", align_bytes=64),
+            placed.tile([P, N], U8, name="k_scales1", align_bytes=64, offset=WINDOW_BYTES),
+        ]
+
+        def quantize_keys(b):
             nc.vector.quantize_mx(out=k_codes[b][:].bitcast(FP8X4), scales=k_scales[b][:], in_=k_listed[b][:])
 
-        q_listed = [keep.tile([P, NQ * PACK], BF16, name=f"q_listed{b}", align_bytes=64) for b in range(B)]
+        quantize_keys(0)
+
+        q_listed = [
+            placed.tile([P, NQ * PACK], BF16, name="q_listed0", align_bytes=64, offset=WINDOW_BYTES),
+            keep.tile([P, NQ * PACK], BF16, name="q_listed1", align_bytes=64),
+        ]
         for t in range(PACK):
             if t < 2:
                 q_pool = keep.tile([P, TQ], BF16, name=f"q_pool{t}")
@@ -119,6 +131,8 @@ def tile_attend_bothw_f_kernel(tc, qT, kT, kb, offq, offs, out):
                 stop=True,
             )
             scores.append(acc)
+            if b == 0:
+                quantize_keys(1)
 
         z = []
         for b in range(B):

@@ -20,7 +20,6 @@ AX = mybir.AxisListType
 
 P = 128
 PACK = 4
-KB_COLS = T // P
 WINDOW_BYTES = 4 * T
 LISTED_BYTES = 2 * N * PACK
 LISTED_AT = WINDOW_BYTES + 2 * NQ * PACK
@@ -35,18 +34,17 @@ def tile_attend_bothw_f_kernel(tc, qT, kT, kb, offq, offs, out):
 
         key_list = keep.tile([P, B * N // 16], U16, name="key_list")
         query_list = keep.tile([P, B * NQ // 16], U16, name="query_list")
-        bias_row = keep.tile([P, KB_COLS], F32, name="bias_row")
+        bias_row = keep.tile([1, T], F32, name="bias_row")
         k_rows = kT.rearrange("(p t) c -> p t c", t=PACK)
         q_rows = qT.rearrange("(p t) c -> p t c", t=PACK)
 
-        nc.sync.dma_start(bias_row[:], kb[0:1, :].rearrange("o (p j) -> (o p) j", j=KB_COLS))
+        nc.sync.dma_start(bias_row[:], kb[0:1, :])
+        nc.sync.dma_start(key_list[:], offs)
         k_raw = []
         for t in range(PACK):
             raw = keep.tile([P, T], F32, name=f"k_raw{t}")
             nc.sync.dma_start(raw[:], k_rows[:, t, :])
             k_raw.append(raw)
-            if t == 0:
-                nc.sync.dma_start(key_list[:], offs)
             if t == 2:
                 nc.sync.dma_start(query_list[:], offq)
         q_raw = []
@@ -55,24 +53,35 @@ def tile_attend_bothw_f_kernel(tc, qT, kT, kb, offq, offs, out):
             nc.sync.dma_start(raw[:], q_rows[:, t, :])
             q_raw.append(raw)
 
-        ident = placed.tile([P, P], F32, name="ident", offset=LISTED_AT + LISTED_BYTES - 2 * P)
+        bias_pool = keep.tile([P, T], F32, name="bias_pool")
+        nc.gpsimd.memset(bias_pool[:], 0.0)
+        nc.vector.tensor_copy(bias_pool[0:1, :], bias_row[:])
+        bias_listed = keep.tile([P, B * N], F32, name="bias_listed")
+        nc.vector.tensor_copy(bias_listed[:], bias_pool[:].indirect(key_list[:]))
+
+        ident = keep.tile([P, P], F32, name="ident")
         make_identity(nc, ident[:])
-        bias_pool = placed.tile([P, T], F32, name="bias_pool", offset=0)
-        bias_view = bias_pool[:].rearrange("m (p g i) -> m g p i", g=KB_COLS // 4, i=4)
-        for g in range(KB_COLS // 4):
-            spread = psum.tile([P, 4, P], F32, name=f"spread{g}")
-            for i in range(4):
-                j = 4 * g + i
-                nc.tensor.transpose(spread[:, i, :], bias_row[:, j : j + 1].to_broadcast([P, P]), ident[:])
-            nc.scalar.copy(bias_view[:, g], spread[:].rearrange("m i p -> m p i"))
+        blocks = N // P
+        bias_cols = placed.tile([P, B * blocks * 4], F32, name="bias_cols", offset=LISTED_AT + LISTED_BYTES - 64)
+        for b in range(B):
+            turned = psum.tile([P, blocks, P], F32, name=f"turned{b}")
+            for i in range(blocks):
+                j = b * blocks + i
+                nc.tensor.transpose(turned[:, i, :], bias_listed[:, j * P : (j + 1) * P], ident[:])
+            nc.scalar.copy(bias_cols[:, b * 16 : b * 16 + blocks], turned[:, :, 0])
+        bias = keep.tile([P, B * N], F32, name="bias")
+        for b in range(B):
+            spread = psum.tile([P, blocks, P], F32, name=f"spread{b}")
+            for i in range(blocks):
+                j = b * 16 + i
+                nc.tensor.transpose(spread[:, i, :], bias_cols[:, j : j + 1].to_broadcast([P, P]), ident[:])
+            nc.scalar.copy(bias[:, b * N : (b + 1) * N], spread[:].rearrange("m i p -> m (i p)"))
 
         k_low = keep.tile([P, 2 * B * N], BF16, name="k_low")
         nc.vector.tensor_copy(k_low[:, 0 : B * N], k_raw[0][:].indirect(key_list[:]))
-        bias = keep.tile([P, B * N], F32, name="bias")
-        nc.vector.tensor_copy(bias[:], bias_pool[:].indirect(key_list[:]))
         nc.vector.tensor_copy(k_low[:, B * N : 2 * B * N], k_raw[1][:].indirect(key_list[:]))
 
-        k_high = placed.tile([P, 2 * B * N], BF16, name="k_high", offset=0)
+        k_high = keep.tile([P, 2 * B * N], BF16, name="k_high")
         nc.vector.tensor_copy(k_high[:, 0 : B * N], k_raw[2][:].indirect(key_list[:]))
         for b in range(B):
             nc.vector.tensor_copy(

@@ -45,19 +45,22 @@ def tile_attend_bothw_f_kernel(tc, qT, kT, kb, offq, offs, out):
             raw = keep.tile([P, T], F32, name=f"k_raw{t}")
             nc.sync.dma_start(raw[:], k_rows[:, t, :])
             k_raw.append(raw)
-            if t == 2:
-                nc.sync.dma_start(query_list[:], offq)
         q_raw = []
         for t in range(PACK):
             raw = keep.tile([P, TQ], F32, name=f"q_raw{t}")
             nc.sync.dma_start(raw[:], q_rows[:, t, :])
             q_raw.append(raw)
+            if t == 0:
+                nc.sync.dma_start(query_list[:], offq)
 
         bias_pool = keep.tile([P, T], F32, name="bias_pool")
         nc.gpsimd.memset(bias_pool[:], 0.0)
         nc.vector.tensor_copy(bias_pool[0:1, :], bias_row[:])
-        bias_listed = keep.tile([P, B * N], F32, name="bias_listed")
-        nc.vector.tensor_copy(bias_listed[:], bias_pool[:].indirect(key_list[:]))
+        bias_listed = [keep.tile([P, N], F32, name=f"bias_listed{b}") for b in range(B)]
+        for b in range(B):
+            nc.vector.tensor_copy(
+                bias_listed[b][:], bias_pool[:].indirect(key_list[:, b * N // 16 : (b + 1) * N // 16])
+            )
 
         ident = keep.tile([P, P], F32, name="ident")
         make_identity(nc, ident[:])
@@ -66,8 +69,7 @@ def tile_attend_bothw_f_kernel(tc, qT, kT, kb, offq, offs, out):
         for b in range(B):
             turned = psum.tile([P, blocks, P], F32, name=f"turned{b}")
             for i in range(blocks):
-                j = b * blocks + i
-                nc.tensor.transpose(turned[:, i, :], bias_listed[:, j * P : (j + 1) * P], ident[:])
+                nc.tensor.transpose(turned[:, i, :], bias_listed[b][:, i * P : (i + 1) * P], ident[:])
             nc.scalar.copy(bias_cols[:, b * 16 : b * 16 + blocks], turned[:, :, 0])
         bias = keep.tile([P, B * N], F32, name="bias")
         for b in range(B):
@@ -97,16 +99,25 @@ def tile_attend_bothw_f_kernel(tc, qT, kT, kb, offq, offs, out):
             for b in range(B):
                 words = k_listed[b][:].rearrange("p (c t) -> p c t", t=PACK)
                 copy(words[:, :, 2 * u : 2 * u + 2], pairs[:, b * N : (b + 1) * N, :])
-        k_codes = [keep.tile([P, N], U32, name=f"k_codes{b}", align_bytes=64) for b in range(B)]
+        parts = ((0, 0, N), (1, 0, N // 2), (1, N // 2, N // 2))
+        banks = ((0, 0, N // 2), (0, N // 2, N // 2), (1, 0, N // 2), (2, 0, N // 2))
+        k_codes = [keep.tile([P, w], U32, name=f"k_codes{i}", align_bytes=64) for i, (b, c0, w) in enumerate(parts)]
         k_scales = [
             keep.tile([P, N], U8, name="k_scales0", align_bytes=64),
-            placed.tile([P, N], U8, name="k_scales1", align_bytes=64, offset=WINDOW_BYTES),
+            keep.tile([P, N // 2], U8, name="k_scales1", align_bytes=64),
+            placed.tile([P, N // 2], U8, name="k_scales2", align_bytes=64, offset=WINDOW_BYTES),
         ]
 
-        def quantize_keys(b):
-            nc.vector.quantize_mx(out=k_codes[b][:].bitcast(FP8X4), scales=k_scales[b][:], in_=k_listed[b][:])
+        def quantize_keys(i):
+            b, c0, w = parts[i]
+            nc.vector.quantize_mx(
+                out=k_codes[i][:].bitcast(FP8X4),
+                scales=k_scales[i][:],
+                in_=k_listed[b][:, c0 * PACK : (c0 + w) * PACK],
+            )
 
         quantize_keys(0)
+        quantize_keys(1)
 
         q_listed = [
             placed.tile([P, NQ * PACK], BF16, name="q_listed0", align_bytes=64, offset=WINDOW_BYTES),
@@ -124,30 +135,26 @@ def tile_attend_bothw_f_kernel(tc, qT, kT, kb, offq, offs, out):
                 else:
                     nc.vector.tensor_copy(dst, q_raw[t][:].indirect(listed))
 
-        scores = []
+        q_codes = [keep.tile([P, NQ], U32, name=f"q_codes{b}", align_bytes=64) for b in range(B)]
+        q_scales = [keep.tile([P, NQ], U8, name=f"q_scales{b}", align_bytes=64) for b in range(B)]
         for b in range(B):
-            q_codes = keep.tile([P, NQ], U32, name=f"q_codes{b}", align_bytes=64)
-            q_scales = keep.tile([P, NQ], U8, name=f"q_scales{b}", align_bytes=64)
-            nc.vector.quantize_mx(out=q_codes[:].bitcast(FP8X4), scales=q_scales[:], in_=q_listed[b][:])
-            acc = psum.tile([P, N], F32, name=f"scores{b}")
+            nc.vector.quantize_mx(out=q_codes[b][:].bitcast(FP8X4), scales=q_scales[b][:], in_=q_listed[b][:])
+        quantize_keys(2)
+        z = [keep.tile([P, N], F32, name=f"z{b}") for b in range(B)]
+        for n, (i, lo, w) in enumerate(banks):
+            b = parts[i][0]
+            c0 = parts[i][1] + lo
+            acc = psum.tile([P, w], F32, name=f"scores{n}")
             nc.tensor.matmul_mx(
                 out=acc[:],
-                lhsT=q_codes[:].bitcast(FP8X4),
-                lhsT_scale=q_scales[:],
-                rhs=k_codes[b][:].bitcast(FP8X4),
-                rhs_scale=k_scales[b][:],
+                lhsT=q_codes[b][:].bitcast(FP8X4),
+                lhsT_scale=q_scales[b][:],
+                rhs=k_codes[i][:, lo : lo + w].bitcast(FP8X4),
+                rhs_scale=k_scales[i][:, lo : lo + w],
                 start=True,
                 stop=True,
             )
-            scores.append(acc)
-            if b == 0:
-                quantize_keys(1)
-
-        z = []
-        for b in range(B):
-            zb = keep.tile([P, N], F32, name=f"z{b}")
-            nc.vector.tensor_tensor(zb[:], scores[b][:], bias[:, b * N : (b + 1) * N], ALU.add)
-            z.append(zb)
+            nc.vector.tensor_tensor(z[b][:, c0 : c0 + w], acc[:], bias[:, b * N + c0 : b * N + c0 + w], ALU.add)
         neg_max = []
         for b in range(B):
             nm = keep.tile([P, 1], F32, name=f"neg_max{b}")
@@ -159,6 +166,9 @@ def tile_attend_bothw_f_kernel(tc, qT, kT, kb, offq, offs, out):
             nc.scalar.activation(e[:], z[b][:], ACT.Exp, bias=neg_max[b][:], scale=1.0, accum_out=total[:])
             inverse = keep.tile([P, 1], F32, name=f"inverse{b}")
             nc.vector.reciprocal(inverse[:], total[:])
-            y = keep.tile([P, N], F32, name=f"y{b}")
-            nc.vector.tensor_scalar(y[:], e[:], inverse[:], None, ALU.mult)
-            nc.sync.dma_start(out[b], y[:])
+            pieces = b + 1
+            for i in range(pieces):
+                cols = slice(i * N // pieces, (i + 1) * N // pieces)
+                y = keep.tile([P, N // pieces], F32, name=f"y{b}_{i}")
+                nc.vector.tensor_scalar(y[:], e[:, cols], inverse[:], None, ALU.mult)
+                nc.sync.dma_start(out[b][:, cols], y[:])

@@ -40,8 +40,10 @@ def tile_attend_bothw_f_kernel(tc, qT, kT, kb, offq, offs, out):
 
         nc.sync.dma_start(bias_row[:], kb[0:1, :])
         nc.sync.dma_start(key_list[:], offs)
-        k_raw = []
-        for t in range(PACK):
+        k_first = keep.tile([P, 2 * T], F32, name="k_first")
+        nc.sync.dma_start(k_first[:], kT.rearrange("(p u t) c -> p u (t c)", u=2, t=2)[:, 0, :])
+        k_raw = [None, None]
+        for t in range(2, PACK):
             raw = keep.tile([P, T], F32, name=f"k_raw{t}")
             nc.sync.dma_start(raw[:], k_rows[:, t, :])
             k_raw.append(raw)
@@ -80,8 +82,13 @@ def tile_attend_bothw_f_kernel(tc, qT, kT, kb, offq, offs, out):
             nc.scalar.copy(bias[:, b * N : (b + 1) * N], spread[:].rearrange("m i p -> m (i p)"))
 
         k_low = keep.tile([P, 2 * B * N], BF16, name="k_low")
-        nc.vector.tensor_copy(k_low[:, 0 : B * N], k_raw[0][:].indirect(key_list[:]))
-        nc.vector.tensor_copy(k_low[:, B * N : 2 * B * N], k_raw[1][:].indirect(key_list[:]))
+        low_planes = k_low[:].rearrange("p (i t c) -> p t i c", i=4, t=2)
+        nc.vector.tensor_copy(low_planes[:, 0], k_first[:, 0:T].indirect(key_list[:]))
+        for b in range(B):
+            nc.vector.tensor_copy(
+                low_planes[:, 1, 2 * b : 2 * b + 2],
+                k_first[:, T : 2 * T].indirect(key_list[:, b * N // 16 : (b + 1) * N // 16]),
+            )
 
         k_high = keep.tile([P, 2 * B * N], BF16, name="k_high")
         nc.vector.tensor_copy(k_high[:, 0 : B * N], k_raw[2][:].indirect(key_list[:]))
@@ -94,11 +101,14 @@ def tile_attend_bothw_f_kernel(tc, qT, kT, kb, offq, offs, out):
             placed.tile([P, N * PACK], BF16, name=f"k_listed{b}", align_bytes=64, offset=LISTED_AT + b * LISTED_BYTES)
             for b in range(B)
         ]
-        for u, (planes, copy) in enumerate(((k_low, nc.scalar.copy), (k_high, nc.vector.tensor_copy))):
-            pairs = planes[:].rearrange("p (t c) -> p c t", t=2)
-            for b in range(B):
-                words = k_listed[b][:].rearrange("p (c t) -> p c t", t=PACK)
-                copy(words[:, :, 2 * u : 2 * u + 2], pairs[:, b * N : (b + 1) * N, :])
+        low_pairs = k_low[:].rearrange("p (i t c) -> p i c t", i=4, t=2)
+        for b, copy in enumerate((nc.scalar.copy, nc.scalar.copy)):
+            words = k_listed[b][:].rearrange("p (i c t) -> p i c t", i=2, t=PACK)
+            copy(words[:, :, :, 0:2], low_pairs[:, 2 * b : 2 * b + 2])
+        high_pairs = k_high[:].rearrange("p (t c) -> p c t", t=2)
+        for b in range(B):
+            words = k_listed[b][:].rearrange("p (c t) -> p c t", t=PACK)
+            nc.vector.tensor_copy(words[:, :, 2:4], high_pairs[:, b * N : (b + 1) * N, :])
         parts = ((0, 0, N), (1, 0, N // 2), (1, N // 2, N // 2))
         banks = ((0, 0, N // 2), (0, N // 2, N // 2), (1, 0, N // 2), (2, 0, N // 2))
         k_codes = [keep.tile([P, w], U32, name=f"k_codes{i}", align_bytes=64) for i, (b, c0, w) in enumerate(parts)]
@@ -166,9 +176,8 @@ def tile_attend_bothw_f_kernel(tc, qT, kT, kb, offq, offs, out):
             nc.scalar.activation(e[:], z[b][:], ACT.Exp, bias=neg_max[b][:], scale=1.0, accum_out=total[:])
             inverse = keep.tile([P, 1], F32, name=f"inverse{b}")
             nc.vector.reciprocal(inverse[:], total[:])
-            pieces = b + 1
-            for i in range(pieces):
-                cols = slice(i * N // pieces, (i + 1) * N // pieces)
-                y = keep.tile([P, N // pieces], F32, name=f"y{b}_{i}")
+            cut = N // 4 if b == 0 else N // 2
+            for i, cols in enumerate((slice(0, cut), slice(cut, N))):
+                y = keep.tile([P, cols.stop - cols.start], F32, name=f"y{b}_{i}")
                 nc.vector.tensor_scalar(y[:], e[:, cols], inverse[:], None, ALU.mult)
                 nc.sync.dma_start(out[b][:, cols], y[:])

@@ -9,7 +9,6 @@ BYTES = 4 * (D * TQ + D * T + T + B * NQ * N) + 2 * 128 * (16 + 64)
 
 F32 = mybir.dt.float32
 BF16 = mybir.dt.bfloat16
-I32 = mybir.dt.int32
 U32 = mybir.dt.uint32
 U16 = mybir.dt.uint16
 U8 = mybir.dt.uint8
@@ -20,9 +19,15 @@ AX = mybir.AxisListType
 
 P = 128
 PACK = 4
-WINDOW_BYTES = 4 * T
-LISTED_BYTES = 2 * N * PACK
-LISTED_AT = WINDOW_BYTES + 2 * NQ * PACK
+GROUP = 16
+HALF = N // 2
+QUERY_BYTES = 2 * NQ * PACK
+KEY_BYTES = 2 * N * PACK
+STRADDLE = 16
+
+
+def entries(listed, first, count):
+    return listed[:, first // GROUP : (first + count) // GROUP]
 
 
 def tile_attend_bothw_f_kernel(tc, qT, kT, kb, offq, offs, out):
@@ -32,8 +37,8 @@ def tile_attend_bothw_f_kernel(tc, qT, kT, kb, offq, offs, out):
         placed = ctx.enter_context(tc.tile_pool(name="placed", bufs=1))
         psum = ctx.enter_context(tc.psum_pool(name="psum", bufs=1))
 
-        key_list = keep.tile([P, B * N // 16], U16, name="key_list")
-        query_list = keep.tile([P, B * NQ // 16], U16, name="query_list")
+        key_list = keep.tile([P, B * N // GROUP], U16, name="key_list")
+        query_list = keep.tile([P, B * NQ // GROUP], U16, name="query_list")
         bias_row = keep.tile([1, T], F32, name="bias_row")
         k_rows = kT.rearrange("(p t) c -> p t c", t=PACK)
         q_rows = qT.rearrange("(p t) c -> p t c", t=PACK)
@@ -42,16 +47,16 @@ def tile_attend_bothw_f_kernel(tc, qT, kT, kb, offq, offs, out):
         nc.sync.dma_start(key_list[:], offs)
         k_first = keep.tile([P, 2 * T], F32, name="k_first")
         nc.sync.dma_start(k_first[:], kT.rearrange("(p u t) c -> p u (t c)", u=2, t=2)[:, 0, :])
-        k_raw = [None, None]
+        k_late = []
         for t in range(2, PACK):
             raw = keep.tile([P, T], F32, name=f"k_raw{t}")
             nc.sync.dma_start(raw[:], k_rows[:, t, :])
-            k_raw.append(raw)
+            k_late.append(raw)
         q_raw = []
         for t in range(PACK):
             raw = keep.tile([P, TQ], F32, name=f"q_raw{t}")
             nc.sync.dma_start(raw[:], q_rows[:, t, :])
-            q_raw.append(raw)
+            q_raw.append(raw[:])
             if t == 0:
                 nc.sync.dma_start(query_list[:], offq)
 
@@ -60,62 +65,60 @@ def tile_attend_bothw_f_kernel(tc, qT, kT, kb, offq, offs, out):
         nc.vector.tensor_copy(bias_pool[0:1, :], bias_row[:])
         bias_listed = [keep.tile([P, N], F32, name=f"bias_listed{b}") for b in range(B)]
         for b in range(B):
-            nc.vector.tensor_copy(
-                bias_listed[b][:], bias_pool[:].indirect(key_list[:, b * N // 16 : (b + 1) * N // 16])
-            )
+            nc.vector.tensor_copy(bias_listed[b][:], bias_pool[:].indirect(entries(key_list, b * N, N)))
 
         ident = keep.tile([P, P], F32, name="ident")
         make_identity(nc, ident[:])
         blocks = N // P
-        bias_cols = placed.tile([P, B * blocks * 4], F32, name="bias_cols", offset=LISTED_AT + LISTED_BYTES - 64)
+        bias_cols = placed.tile(
+            [P, B * STRADDLE], F32, name="bias_cols", offset=QUERY_BYTES + KEY_BYTES - 4 * STRADDLE
+        )
         for b in range(B):
             turned = psum.tile([P, blocks, P], F32, name=f"turned{b}")
             for i in range(blocks):
                 nc.tensor.transpose(turned[:, i, :], bias_listed[b][:, i * P : (i + 1) * P], ident[:])
-            nc.scalar.copy(bias_cols[:, b * 16 : b * 16 + blocks], turned[:, :, 0])
+            nc.scalar.copy(bias_cols[:, b * STRADDLE : b * STRADDLE + blocks], turned[:, :, 0])
         bias = keep.tile([P, B * N], F32, name="bias")
         for b in range(B):
             spread = psum.tile([P, blocks, P], F32, name=f"spread{b}")
             for i in range(blocks):
-                j = b * 16 + i
+                j = b * STRADDLE + i
                 nc.tensor.transpose(spread[:, i, :], bias_cols[:, j : j + 1].to_broadcast([P, P]), ident[:])
             nc.scalar.copy(bias[:, b * N : (b + 1) * N], spread[:].rearrange("m i p -> m (i p)"))
 
         k_low = keep.tile([P, 2 * B * N], BF16, name="k_low")
-        low_planes = k_low[:].rearrange("p (i t c) -> p t i c", i=4, t=2)
+        low_planes = k_low[:].rearrange("p (i t c) -> p t i c", t=2, c=HALF)
         nc.vector.tensor_copy(low_planes[:, 0], k_first[:, 0:T].indirect(key_list[:]))
         for b in range(B):
             nc.vector.tensor_copy(
-                low_planes[:, 1, 2 * b : 2 * b + 2],
-                k_first[:, T : 2 * T].indirect(key_list[:, b * N // 16 : (b + 1) * N // 16]),
+                low_planes[:, 1, 2 * b : 2 * b + 2], k_first[:, T : 2 * T].indirect(entries(key_list, b * N, N))
             )
-
         k_high = keep.tile([P, 2 * B * N], BF16, name="k_high")
-        nc.vector.tensor_copy(k_high[:, 0 : B * N], k_raw[2][:].indirect(key_list[:]))
+        nc.vector.tensor_copy(k_high[:, 0 : B * N], k_late[0][:].indirect(key_list[:]))
         for b in range(B):
             nc.vector.tensor_copy(
-                k_high[:, (B + b) * N : (B + b + 1) * N],
-                k_raw[3][:].indirect(key_list[:, b * N // 16 : (b + 1) * N // 16]),
+                k_high[:, (B + b) * N : (B + b + 1) * N], k_late[1][:].indirect(entries(key_list, b * N, N))
             )
+
         k_listed = [
-            placed.tile([P, N * PACK], BF16, name=f"k_listed{b}", align_bytes=64, offset=LISTED_AT + b * LISTED_BYTES)
+            placed.tile([P, N * PACK], BF16, name=f"k_listed{b}", align_bytes=64, offset=QUERY_BYTES + b * KEY_BYTES)
             for b in range(B)
         ]
-        low_pairs = k_low[:].rearrange("p (i t c) -> p i c t", i=4, t=2)
-        for b, copy in enumerate((nc.scalar.copy, nc.scalar.copy)):
-            words = k_listed[b][:].rearrange("p (i c t) -> p i c t", i=2, t=PACK)
-            copy(words[:, :, :, 0:2], low_pairs[:, 2 * b : 2 * b + 2])
+        low_pairs = k_low[:].rearrange("p (i t c) -> p i c t", t=2, c=HALF)
+        for b in range(B):
+            by_half = k_listed[b][:].rearrange("p (i c t) -> p i c t", c=HALF, t=PACK)
+            nc.scalar.copy(by_half[:, :, :, 0:2], low_pairs[:, 2 * b : 2 * b + 2])
         high_pairs = k_high[:].rearrange("p (t c) -> p c t", t=2)
         for b in range(B):
-            words = k_listed[b][:].rearrange("p (c t) -> p c t", t=PACK)
-            nc.vector.tensor_copy(words[:, :, 2:4], high_pairs[:, b * N : (b + 1) * N, :])
-        parts = ((0, 0, N), (1, 0, N // 2), (1, N // 2, N // 2))
-        banks = ((0, 0, N // 2), (0, N // 2, N // 2), (1, 0, N // 2), (2, 0, N // 2))
+            by_slot = k_listed[b][:].rearrange("p (c t) -> p c t", t=PACK)
+            nc.vector.tensor_copy(by_slot[:, :, 2:4], high_pairs[:, b * N : (b + 1) * N, :])
+
+        parts = ((0, 0, N), (1, 0, HALF), (1, HALF, HALF))
         k_codes = [keep.tile([P, w], U32, name=f"k_codes{i}", align_bytes=64) for i, (b, c0, w) in enumerate(parts)]
         k_scales = [
             keep.tile([P, N], U8, name="k_scales0", align_bytes=64),
-            keep.tile([P, N // 2], U8, name="k_scales1", align_bytes=64),
-            placed.tile([P, N // 2], U8, name="k_scales2", align_bytes=64, offset=WINDOW_BYTES),
+            keep.tile([P, HALF], U8, name="k_scales1", align_bytes=64),
+            placed.tile([P, HALF], U8, name="k_scales2", align_bytes=64, offset=0),
         ]
 
         def quantize_keys(i):
@@ -130,41 +133,45 @@ def tile_attend_bothw_f_kernel(tc, qT, kT, kb, offq, offs, out):
         quantize_keys(1)
 
         q_listed = [
-            placed.tile([P, NQ * PACK], BF16, name="q_listed0", align_bytes=64, offset=WINDOW_BYTES),
+            placed.tile([P, NQ * PACK], BF16, name="q_listed0", align_bytes=64, offset=0),
             keep.tile([P, NQ * PACK], BF16, name="q_listed1", align_bytes=64),
         ]
         for t in range(PACK):
             if t < 2:
                 q_pool = keep.tile([P, TQ], BF16, name=f"q_pool{t}")
-                nc.scalar.copy(q_pool[:], q_raw[t][:])
+                nc.scalar.copy(q_pool[:], q_raw[t])
             for b in range(B):
                 dst = q_listed[b][:].rearrange("p (c t) -> p t c", t=PACK)[:, t]
-                listed = query_list[:, b * NQ // 16 : (b + 1) * NQ // 16]
+                listed = entries(query_list, b * NQ, NQ)
                 if t < 2:
                     nc.scalar.activation(dst, q_pool[:].indirect(listed), ACT.Copy)
                 else:
-                    nc.vector.tensor_copy(dst, q_raw[t][:].indirect(listed))
+                    nc.vector.tensor_copy(dst, q_raw[t].indirect(listed))
 
         q_codes = [keep.tile([P, NQ], U32, name=f"q_codes{b}", align_bytes=64) for b in range(B)]
         q_scales = [keep.tile([P, NQ], U8, name=f"q_scales{b}", align_bytes=64) for b in range(B)]
         for b in range(B):
             nc.vector.quantize_mx(out=q_codes[b][:].bitcast(FP8X4), scales=q_scales[b][:], in_=q_listed[b][:])
         quantize_keys(2)
+
         z = [keep.tile([P, N], F32, name=f"z{b}") for b in range(B)]
-        for n, (i, lo, w) in enumerate(banks):
+        for n, (i, lo) in enumerate(((0, 0), (0, HALF), (1, 0), (2, 0))):
             b = parts[i][0]
             c0 = parts[i][1] + lo
-            acc = psum.tile([P, w], F32, name=f"scores{n}")
+            acc = psum.tile([P, HALF], F32, name=f"scores{n}")
             nc.tensor.matmul_mx(
                 out=acc[:],
                 lhsT=q_codes[b][:].bitcast(FP8X4),
                 lhsT_scale=q_scales[b][:],
-                rhs=k_codes[i][:, lo : lo + w].bitcast(FP8X4),
-                rhs_scale=k_scales[i][:, lo : lo + w],
+                rhs=k_codes[i][:, lo : lo + HALF].bitcast(FP8X4),
+                rhs_scale=k_scales[i][:, lo : lo + HALF],
                 start=True,
                 stop=True,
             )
-            nc.vector.tensor_tensor(z[b][:, c0 : c0 + w], acc[:], bias[:, b * N + c0 : b * N + c0 + w], ALU.add)
+            nc.vector.tensor_tensor(
+                z[b][:, c0 : c0 + HALF], acc[:], bias[:, b * N + c0 : b * N + c0 + HALF], ALU.add
+            )
+
         neg_max = []
         for b in range(B):
             nm = keep.tile([P, 1], F32, name=f"neg_max{b}")
@@ -176,7 +183,7 @@ def tile_attend_bothw_f_kernel(tc, qT, kT, kb, offq, offs, out):
             nc.scalar.activation(e[:], z[b][:], ACT.Exp, bias=neg_max[b][:], scale=1.0, accum_out=total[:])
             inverse = keep.tile([P, 1], F32, name=f"inverse{b}")
             nc.vector.reciprocal(inverse[:], total[:])
-            cut = N // 4 if b == 0 else N // 2
+            cut = N // 4 if b == 0 else HALF
             for i, cols in enumerate((slice(0, cut), slice(cut, N))):
                 y = keep.tile([P, cols.stop - cols.start], F32, name=f"y{b}_{i}")
                 nc.vector.tensor_scalar(y[:], e[:, cols], inverse[:], None, ALU.mult)

@@ -23,11 +23,21 @@ GROUP = 16
 HALF = N // 2
 QUERY_BYTES = 2 * NQ * PACK
 KEY_BYTES = 2 * N * PACK
-STRADDLE = 16
 
 
 def entries(listed, first, count):
     return listed[:, first // GROUP : (first + count) // GROUP]
+
+
+def gather(nc, on_scalar, out, window, listed):
+    if on_scalar:
+        nc.scalar.activation(out, window.indirect(listed), ACT.Copy)
+    else:
+        nc.vector.tensor_copy(out, window.indirect(listed))
+
+
+def place(copy, out, src):
+    copy(out, src)
 
 
 def tile_attend_bothw_f_kernel(tc, qT, kT, kb, offq, offs, out):
@@ -44,14 +54,13 @@ def tile_attend_bothw_f_kernel(tc, qT, kT, kb, offq, offs, out):
         q_rows = qT.rearrange("(p t) c -> p t c", t=PACK)
 
         nc.sync.dma_start(bias_row[:], kb[0:1, :])
-        nc.sync.dma_start(key_list[:], offs)
-        k_first = keep.tile([P, 2 * T], F32, name="k_first")
-        nc.sync.dma_start(k_first[:], kT.rearrange("(p u t) c -> p u (t c)", u=2, t=2)[:, 0, :])
-        k_late = []
-        for t in range(2, PACK):
+        k_raw = []
+        for t in range(PACK):
             raw = keep.tile([P, T], F32, name=f"k_raw{t}")
             nc.sync.dma_start(raw[:], k_rows[:, t, :])
-            k_late.append(raw)
+            k_raw.append(raw[:])
+            if t == 0:
+                nc.sync.dma_start(key_list[:], offs)
         q_raw = []
         for t in range(PACK):
             raw = keep.tile([P, TQ], F32, name=f"q_raw{t}")
@@ -65,112 +74,88 @@ def tile_attend_bothw_f_kernel(tc, qT, kT, kb, offq, offs, out):
         nc.vector.tensor_copy(bias_pool[0:1, :], bias_row[:])
         bias_listed = [keep.tile([P, N], F32, name=f"bias_listed{b}") for b in range(B)]
         for b in range(B):
-            nc.vector.tensor_copy(bias_listed[b][:], bias_pool[:].indirect(entries(key_list, b * N, N)))
+            gather(nc, False, bias_listed[b][:], bias_pool[:], entries(key_list, b * N, N))
 
         ident = keep.tile([P, P], F32, name="ident")
         make_identity(nc, ident[:])
         blocks = N // P
-        bias_cols = placed.tile(
-            [P, B * STRADDLE], F32, name="bias_cols", offset=QUERY_BYTES + KEY_BYTES - 4 * STRADDLE
-        )
+        bias_cols = keep.tile([P, B * blocks], F32, name="bias_cols")
         for b in range(B):
             turned = psum.tile([P, blocks, P], F32, name=f"turned{b}")
             for i in range(blocks):
                 nc.tensor.transpose(turned[:, i, :], bias_listed[b][:, i * P : (i + 1) * P], ident[:])
-            nc.scalar.copy(bias_cols[:, b * STRADDLE : b * STRADDLE + blocks], turned[:, :, 0])
-        bias = keep.tile([P, B * N], F32, name="bias")
+            nc.scalar.copy(bias_cols[:, b * blocks : (b + 1) * blocks], turned[:, :, 0])
+        spreads = []
         for b in range(B):
             spread = psum.tile([P, blocks, P], F32, name=f"spread{b}")
             for i in range(blocks):
-                j = b * STRADDLE + i
+                j = b * blocks + i
                 nc.tensor.transpose(spread[:, i, :], bias_cols[:, j : j + 1].to_broadcast([P, P]), ident[:])
-            nc.scalar.copy(bias[:, b * N : (b + 1) * N], spread[:].rearrange("m i p -> m (i p)"))
+            spreads.append(spread)
 
-        k_low = keep.tile([P, 2 * B * N], BF16, name="k_low")
-        low_planes = k_low[:].rearrange("p (i t c) -> p t i c", t=2, c=HALF)
-        nc.vector.tensor_copy(low_planes[:, 0], k_first[:, 0:T].indirect(key_list[:]))
-        for b in range(B):
-            nc.vector.tensor_copy(
-                low_planes[:, 1, 2 * b : 2 * b + 2], k_first[:, T : 2 * T].indirect(entries(key_list, b * N, N))
-            )
-        k_high = keep.tile([P, 2 * B * N], BF16, name="k_high")
-        nc.vector.tensor_copy(k_high[:, 0 : B * N], k_late[0][:].indirect(key_list[:]))
-        for b in range(B):
-            nc.vector.tensor_copy(
-                k_high[:, (B + b) * N : (B + b + 1) * N], k_late[1][:].indirect(entries(key_list, b * N, N))
-            )
-
+        k_pairs = [keep.tile([P, 2 * B * N], BF16, name=f"k_pairs{u}") for u in range(2)]
         k_listed = [
-            placed.tile([P, N * PACK], BF16, name=f"k_listed{b}", align_bytes=64, offset=QUERY_BYTES + b * KEY_BYTES)
+            placed.tile([P, N * PACK], BF16, name=f"k_listed{b}", align_bytes=64, offset=b * KEY_BYTES)
             for b in range(B)
         ]
-        low_pairs = k_low[:].rearrange("p (i t c) -> p i c t", t=2, c=HALF)
+        by_half = [k_listed[b][:].rearrange("p (i c t) -> p i c t", c=HALF, t=PACK) for b in range(B)]
+        low, high = [k_pairs[u][:].rearrange("p (t i c) -> p i c t", t=2, c=HALF) for u in range(2)]
+        for t in range(2):
+            gather(nc, False, k_pairs[0][:, t * B * N : (t + 1) * B * N], k_raw[t], key_list[:])
         for b in range(B):
-            by_half = k_listed[b][:].rearrange("p (i c t) -> p i c t", c=HALF, t=PACK)
-            nc.scalar.copy(by_half[:, :, :, 0:2], low_pairs[:, 2 * b : 2 * b + 2])
-        high_pairs = k_high[:].rearrange("p (t c) -> p c t", t=2)
+            place(nc.vector.tensor_copy, by_half[b][:, :, :, 0:2], low[:, 2 * b : 2 * b + 2])
+        bias = keep.tile([P, B * N], F32, name="bias")
         for b in range(B):
-            by_slot = k_listed[b][:].rearrange("p (c t) -> p c t", t=PACK)
-            nc.vector.tensor_copy(by_slot[:, :, 2:4], high_pairs[:, b * N : (b + 1) * N, :])
-
-        parts = ((0, 0, N), (1, 0, HALF), (1, HALF, HALF))
-        k_codes = [keep.tile([P, w], U32, name=f"k_codes{i}", align_bytes=64) for i, (b, c0, w) in enumerate(parts)]
-        k_scales = [
-            keep.tile([P, N], U8, name="k_scales0", align_bytes=64),
-            keep.tile([P, HALF], U8, name="k_scales1", align_bytes=64),
-            placed.tile([P, HALF], U8, name="k_scales2", align_bytes=64, offset=0),
-        ]
-
-        def quantize_keys(i):
-            b, c0, w = parts[i]
+            nc.vector.tensor_copy(bias[:, b * N : (b + 1) * N], spreads[b][:].rearrange("m i p -> m (i p)"))
+        gather(nc, True, k_pairs[1][:, 0 : B * N], k_raw[2], key_list[:])
+        for i0, n in ((0, 1), (1, 1), (2, 2)):
+            run = k_pairs[1][:, B * N + i0 * HALF : B * N + (i0 + n) * HALF]
+            gather(nc, True, run, k_raw[3], entries(key_list, i0 * HALF, n * HALF))
+            place(nc.vector.tensor_copy, by_half[i0 // 2][:, i0 % 2 : i0 % 2 + n, :, 2:4], high[:, i0 : i0 + n])
+        k_codes = keep.tile([P, B * N], U32, name="k_codes", align_bytes=64)
+        k_scales = keep.tile([P, B * N], U8, name="k_scales", align_bytes=64)
+        for b in range(B):
             nc.vector.quantize_mx(
-                out=k_codes[i][:].bitcast(FP8X4),
-                scales=k_scales[i][:],
-                in_=k_listed[b][:, c0 * PACK : (c0 + w) * PACK],
+                out=k_codes[:, b * N : (b + 1) * N].bitcast(FP8X4),
+                scales=k_scales[:, b * N : (b + 1) * N],
+                in_=k_listed[b][:],
             )
 
-        quantize_keys(0)
-        quantize_keys(1)
-
-        q_listed = [
-            placed.tile([P, NQ * PACK], BF16, name="q_listed0", align_bytes=64, offset=0),
-            keep.tile([P, NQ * PACK], BF16, name="q_listed1", align_bytes=64),
-        ]
-        for t in range(PACK):
-            if t < 2:
-                q_pool = keep.tile([P, TQ], BF16, name=f"q_pool{t}")
-                nc.scalar.copy(q_pool[:], q_raw[t])
-            for b in range(B):
-                dst = q_listed[b][:].rearrange("p (c t) -> p t c", t=PACK)[:, t]
-                listed = entries(query_list, b * NQ, NQ)
-                if t < 2:
-                    nc.scalar.activation(dst, q_pool[:].indirect(listed), ACT.Copy)
-                else:
-                    nc.vector.tensor_copy(dst, q_raw[t].indirect(listed))
-
+        last = PACK - 1
+        q_runs = keep.tile([P, PACK, B * NQ], BF16, name="q_runs")
+        for t in range(last):
+            gather(nc, True, q_runs[:, t, :], q_raw[t], query_list[:])
+        gather(nc, True, q_runs[:, last, NQ:], q_raw[last], entries(query_list, NQ, NQ))
+        q_listed = placed.tile([P, B * NQ * PACK], BF16, name="q_listed", align_bytes=64, offset=0)
+        q_words = q_listed[:].rearrange("p (c t) -> p c t", t=PACK)
+        nc.vector.tensor_copy(q_words[:, :, 0:last], q_runs[:, 0:last, :].rearrange("p t c -> p c t"))
+        gather(nc, False, q_words[:, 0:NQ, last], q_raw[last], entries(query_list, 0, NQ))
         q_codes = [keep.tile([P, NQ], U32, name=f"q_codes{b}", align_bytes=64) for b in range(B)]
         q_scales = [keep.tile([P, NQ], U8, name=f"q_scales{b}", align_bytes=64) for b in range(B)]
         for b in range(B):
-            nc.vector.quantize_mx(out=q_codes[b][:].bitcast(FP8X4), scales=q_scales[b][:], in_=q_listed[b][:])
-        quantize_keys(2)
+            if b == 1:
+                nc.vector.tensor_copy(q_words[:, NQ:, last], q_runs[:, last, NQ:])
+            nc.vector.quantize_mx(
+                out=q_codes[b][:].bitcast(FP8X4),
+                scales=q_scales[b][:],
+                in_=q_listed[:, b * NQ * PACK : (b + 1) * NQ * PACK],
+            )
 
         z = [keep.tile([P, N], F32, name=f"z{b}") for b in range(B)]
-        for n, (i, lo) in enumerate(((0, 0), (0, HALF), (1, 0), (2, 0))):
-            b = parts[i][0]
-            c0 = parts[i][1] + lo
+        for n in range(2 * B):
+            b, c0 = n // 2, n % 2 * HALF
+            cols = slice(n * HALF, (n + 1) * HALF)
             acc = psum.tile([P, HALF], F32, name=f"scores{n}")
             nc.tensor.matmul_mx(
                 out=acc[:],
                 lhsT=q_codes[b][:].bitcast(FP8X4),
                 lhsT_scale=q_scales[b][:],
-                rhs=k_codes[i][:, lo : lo + HALF].bitcast(FP8X4),
-                rhs_scale=k_scales[i][:, lo : lo + HALF],
+                rhs=k_codes[:, cols].bitcast(FP8X4),
+                rhs_scale=k_scales[:, cols],
                 start=True,
                 stop=True,
             )
-            nc.vector.tensor_tensor(
-                z[b][:, c0 : c0 + HALF], acc[:], bias[:, b * N + c0 : b * N + c0 + HALF], ALU.add
-            )
+            nc.vector.tensor_tensor(z[b][:, c0 : c0 + HALF], acc[:], bias[:, cols], ALU.add)
 
         neg_max = []
         for b in range(B):

@@ -50,16 +50,16 @@ def tile_attend_bothw_f_kernel(tc, qT, kT, kb, offq, offs, out):
         key_list = keep.tile([P, B * N // GROUP], U16, name="key_list")
         query_list = keep.tile([P, B * NQ // GROUP], U16, name="query_list")
         bias_row = keep.tile([1, T], F32, name="bias_row")
-        k_rows = kT.rearrange("(p t) c -> p t c", t=PACK)
+        k_rows = kT.rearrange("(p t) c -> p (t c)", t=PACK)
         q_rows = qT.rearrange("(p t) c -> p t c", t=PACK)
 
         nc.sync.dma_start(bias_row[:], kb[0:1, :])
         k_raw = []
-        for t in range(PACK):
-            raw = keep.tile([P, T], F32, name=f"k_raw{t}")
-            nc.sync.dma_start(raw[:], k_rows[:, t, :])
-            k_raw.append(raw[:])
-            if t == 0:
+        for t0, n in ((0, 1), (1, 2), (3, 1)):
+            raw = keep.tile([P, n * T], F32, name=f"k_raw{t0}")
+            nc.sync.dma_start(raw[:], k_rows[:, t0 * T : (t0 + n) * T])
+            k_raw.extend(raw[:, i * T : (i + 1) * T] for i in range(n))
+            if t0 == 0:
                 nc.sync.dma_start(key_list[:], offs)
         q_raw = []
         for t in range(PACK):
@@ -93,21 +93,23 @@ def tile_attend_bothw_f_kernel(tc, qT, kT, kb, offq, offs, out):
                 nc.tensor.transpose(spread[:, i, :], bias_cols[:, j : j + 1].to_broadcast([P, P]), ident[:])
             spreads.append(spread)
 
-        k_pairs = [keep.tile([P, 2 * B * N], BF16, name=f"k_pairs{u}") for u in range(2)]
+        k_pairs = [keep.tile([P, 2 * B * N], (BF16, F32)[u], name=f"k_pairs{u}") for u in range(2)]
         k_listed = [
             placed.tile([P, N * PACK], BF16, name=f"k_listed{b}", align_bytes=64, offset=b * KEY_BYTES)
             for b in range(B)
         ]
         by_half = [k_listed[b][:].rearrange("p (i c t) -> p i c t", c=HALF, t=PACK) for b in range(B)]
-        low, high = [k_pairs[u][:].rearrange("p (t i c) -> p i c t", t=2, c=HALF) for u in range(2)]
+        low = k_pairs[0][:].rearrange("p (i t c) -> p i c t", t=2, c=HALF)
+        high = k_pairs[1][:].rearrange("p (t i c) -> p i c t", t=2, c=HALF)
+        low_planes = k_pairs[0][:].rearrange("p (i t c) -> p t i c", t=2, c=HALF)
         for t in range(2):
-            gather(nc, False, k_pairs[0][:, t * B * N : (t + 1) * B * N], k_raw[t], key_list[:])
+            gather(nc, False, low_planes[:, t], k_raw[t], key_list[:])
         for b in range(B):
             place(nc.vector.tensor_copy, by_half[b][:, :, :, 0:2], low[:, 2 * b : 2 * b + 2])
+        gather(nc, True, k_pairs[1][:, 0 : B * N], k_raw[2], key_list[:])
         bias = keep.tile([P, B * N], F32, name="bias")
         for b in range(B):
-            nc.vector.tensor_copy(bias[:, b * N : (b + 1) * N], spreads[b][:].rearrange("m i p -> m (i p)"))
-        gather(nc, True, k_pairs[1][:, 0 : B * N], k_raw[2], key_list[:])
+            nc.scalar.copy(bias[:, b * N : (b + 1) * N], spreads[b][:].rearrange("m i p -> m (i p)"))
         for i0, n in ((0, 1), (1, 1), (2, 2)):
             run = k_pairs[1][:, B * N + i0 * HALF : B * N + (i0 + n) * HALF]
             gather(nc, True, run, k_raw[3], entries(key_list, i0 * HALF, n * HALF))
@@ -123,18 +125,21 @@ def tile_attend_bothw_f_kernel(tc, qT, kT, kb, offq, offs, out):
 
         last = PACK - 1
         q_runs = keep.tile([P, PACK, B * NQ], BF16, name="q_runs")
-        for t in range(last):
+        for t in range(2):
             gather(nc, True, q_runs[:, t, :], q_raw[t], query_list[:])
-        gather(nc, True, q_runs[:, last, NQ:], q_raw[last], entries(query_list, NQ, NQ))
+        for t, b in ((2, 0), (2, 1), (last, 1)):
+            gather(nc, True, q_runs[:, t, b * NQ : (b + 1) * NQ], q_raw[t], entries(query_list, b * NQ, NQ))
         q_listed = placed.tile([P, B * NQ * PACK], BF16, name="q_listed", align_bytes=64, offset=0)
         q_words = q_listed[:].rearrange("p (c t) -> p c t", t=PACK)
-        nc.vector.tensor_copy(q_words[:, :, 0:last], q_runs[:, 0:last, :].rearrange("p t c -> p c t"))
+        q_planes = q_runs[:].rearrange("p t c -> p c t")
+        nc.vector.tensor_copy(q_words[:, NQ:, 0:2], q_planes[:, NQ:, 0:2])
+        nc.vector.tensor_copy(q_words[:, 0:NQ, 0:last], q_planes[:, 0:NQ, 0:last])
         gather(nc, False, q_words[:, 0:NQ, last], q_raw[last], entries(query_list, 0, NQ))
         q_codes = [keep.tile([P, NQ], U32, name=f"q_codes{b}", align_bytes=64) for b in range(B)]
         q_scales = [keep.tile([P, NQ], U8, name=f"q_scales{b}", align_bytes=64) for b in range(B)]
         for b in range(B):
             if b == 1:
-                nc.vector.tensor_copy(q_words[:, NQ:, last], q_runs[:, last, NQ:])
+                nc.vector.tensor_copy(q_words[:, NQ:, 2:4], q_planes[:, NQ:, 2:4])
             nc.vector.quantize_mx(
                 out=q_codes[b][:].bitcast(FP8X4),
                 scales=q_scales[b][:],

@@ -51,20 +51,19 @@ def tile_attend_bothw_f_kernel(tc, qT, kT, kb, offq, offs, out):
         query_list = keep.tile([P, B * NQ // GROUP], U16, name="query_list")
         bias_row = keep.tile([1, T], F32, name="bias_row")
         k_rows = kT.rearrange("(p t) c -> p (t c)", t=PACK)
-        q_rows = qT.rearrange("(p t) c -> p t c", t=PACK)
+        q_rows = qT.rearrange("(p t) c -> p (t c)", t=PACK)
 
         nc.sync.dma_start(bias_row[:], kb[0:1, :])
+        nc.sync.dma_start(key_list[:], offs)
         k_raw = []
-        for t0, n in ((0, 1), (1, 2), (3, 1)):
+        for t0, n in ((0, 2), (2, 1), (3, 1)):
             raw = keep.tile([P, n * T], F32, name=f"k_raw{t0}")
             nc.sync.dma_start(raw[:], k_rows[:, t0 * T : (t0 + n) * T])
             k_raw.extend(raw[:, i * T : (i + 1) * T] for i in range(n))
-            if t0 == 0:
-                nc.sync.dma_start(key_list[:], offs)
         q_raw = []
         for t in range(PACK):
             raw = keep.tile([P, TQ], F32, name=f"q_raw{t}")
-            nc.sync.dma_start(raw[:], q_rows[:, t, :])
+            nc.sync.dma_start(raw[:], q_rows[:, t * TQ : (t + 1) * TQ])
             q_raw.append(raw[:])
             if t == 0:
                 nc.sync.dma_start(query_list[:], offq)
@@ -85,15 +84,15 @@ def tile_attend_bothw_f_kernel(tc, qT, kT, kb, offq, offs, out):
             for i in range(blocks):
                 nc.tensor.transpose(turned[:, i, :], bias_listed[b][:, i * P : (i + 1) * P], ident[:])
             nc.scalar.copy(bias_cols[:, b * blocks : (b + 1) * blocks], turned[:, :, 0])
-        spreads = []
+        bias = keep.tile([P, B * N], F32, name="bias")
         for b in range(B):
             spread = psum.tile([P, blocks, P], F32, name=f"spread{b}")
             for i in range(blocks):
                 j = b * blocks + i
                 nc.tensor.transpose(spread[:, i, :], bias_cols[:, j : j + 1].to_broadcast([P, P]), ident[:])
-            spreads.append(spread)
+            nc.scalar.copy(bias[:, b * N : (b + 1) * N], spread[:].rearrange("m i p -> m (i p)"))
 
-        k_pairs = [keep.tile([P, 2 * B * N], (BF16, F32)[u], name=f"k_pairs{u}") for u in range(2)]
+        k_pairs = [keep.tile([P, 2 * B * N], BF16, name=f"k_pairs{u}") for u in range(2)]
         k_listed = [
             placed.tile([P, N * PACK], BF16, name=f"k_listed{b}", align_bytes=64, offset=b * KEY_BYTES)
             for b in range(B)
@@ -107,47 +106,56 @@ def tile_attend_bothw_f_kernel(tc, qT, kT, kb, offq, offs, out):
         for b in range(B):
             place(nc.vector.tensor_copy, by_half[b][:, :, :, 0:2], low[:, 2 * b : 2 * b + 2])
         gather(nc, True, k_pairs[1][:, 0 : B * N], k_raw[2], key_list[:])
-        bias = keep.tile([P, B * N], F32, name="bias")
-        for b in range(B):
-            nc.scalar.copy(bias[:, b * N : (b + 1) * N], spreads[b][:].rearrange("m i p -> m (i p)"))
-        for i0, n in ((0, 1), (1, 1), (2, 2)):
-            run = k_pairs[1][:, B * N + i0 * HALF : B * N + (i0 + n) * HALF]
-            gather(nc, True, run, k_raw[3], entries(key_list, i0 * HALF, n * HALF))
-            place(nc.vector.tensor_copy, by_half[i0 // 2][:, i0 % 2 : i0 % 2 + n, :, 2:4], high[:, i0 : i0 + n])
-        k_codes = keep.tile([P, B * N], U32, name="k_codes", align_bytes=64)
-        k_scales = keep.tile([P, B * N], U8, name="k_scales", align_bytes=64)
-        for b in range(B):
+        for i in range(2):
+            run = k_pairs[1][:, B * N + i * HALF : B * N + (i + 1) * HALF]
+            gather(nc, False, run, k_raw[3], entries(key_list, i * HALF, HALF))
+        gather(nc, True, k_pairs[1][:, (B + 1) * N :], k_raw[3], entries(key_list, N, N))
+        for i in range(2):
+            place(nc.vector.tensor_copy, by_half[0][:, i : i + 1, :, 2:4], high[:, i : i + 1])
+        place(nc.vector.tensor_copy, by_half[1][:, :, :, 2:4], high[:, 2:4])
+
+        parts = ((0, 0, N), (1, 0, HALF), (1, HALF, HALF))
+        k_codes = [keep.tile([P, w], U32, name=f"k_codes{i}", align_bytes=64) for i, (b, c0, w) in enumerate(parts)]
+        k_scales = [
+            keep.tile([P, N], U8, name="k_scales0", align_bytes=64),
+            keep.tile([P, HALF], U8, name="k_scales1", align_bytes=64),
+            placed.tile([P, HALF], U8, name="k_scales2", align_bytes=64, offset=B * KEY_BYTES),
+        ]
+
+        def quantize_keys(i):
+            b, c0, w = parts[i]
             nc.vector.quantize_mx(
-                out=k_codes[:, b * N : (b + 1) * N].bitcast(FP8X4),
-                scales=k_scales[:, b * N : (b + 1) * N],
-                in_=k_listed[b][:],
+                out=k_codes[i][:].bitcast(FP8X4),
+                scales=k_scales[i][:],
+                in_=k_listed[b][:, c0 * PACK : (c0 + w) * PACK],
             )
 
-        last = PACK - 1
-        q_runs = keep.tile([P, PACK, B * NQ], BF16, name="q_runs")
+        quantize_keys(0)
+        quantize_keys(1)
+
+        q_listed = [
+            placed.tile([P, NQ * PACK], BF16, name="q_listed0", align_bytes=64, offset=B * KEY_BYTES),
+            keep.tile([P, NQ * PACK], BF16, name="q_listed1", align_bytes=64),
+        ]
+        q_words = [q_listed[b][:].rearrange("p (c t) -> p c t", t=PACK) for b in range(B)]
+        q_runs = keep.tile([P, 2, B * NQ], BF16, name="q_runs")
         for t in range(2):
             gather(nc, True, q_runs[:, t, :], q_raw[t], query_list[:])
-        for t, b in ((2, 0), (2, 1), (last, 1)):
-            gather(nc, True, q_runs[:, t, b * NQ : (b + 1) * NQ], q_raw[t], entries(query_list, b * NQ, NQ))
-        q_listed = placed.tile([P, B * NQ * PACK], BF16, name="q_listed", align_bytes=64, offset=0)
-        q_words = q_listed[:].rearrange("p (c t) -> p c t", t=PACK)
         q_planes = q_runs[:].rearrange("p t c -> p c t")
-        nc.vector.tensor_copy(q_words[:, NQ:, 0:2], q_planes[:, NQ:, 0:2])
-        nc.vector.tensor_copy(q_words[:, 0:NQ, 0:last], q_planes[:, 0:NQ, 0:last])
-        gather(nc, False, q_words[:, 0:NQ, last], q_raw[last], entries(query_list, 0, NQ))
+        for b in range(B):
+            nc.scalar.copy(q_words[b][:, :, 0:2], q_planes[:, b * NQ : (b + 1) * NQ, :])
+        for t in range(2, PACK):
+            for b in range(B):
+                gather(nc, False, q_words[b][:, :, t], q_raw[t], entries(query_list, b * NQ, NQ))
+
         q_codes = [keep.tile([P, NQ], U32, name=f"q_codes{b}", align_bytes=64) for b in range(B)]
         q_scales = [keep.tile([P, NQ], U8, name=f"q_scales{b}", align_bytes=64) for b in range(B)]
         for b in range(B):
-            if b == 1:
-                nc.vector.tensor_copy(q_words[:, NQ:, 2:4], q_planes[:, NQ:, 2:4])
-            nc.vector.quantize_mx(
-                out=q_codes[b][:].bitcast(FP8X4),
-                scales=q_scales[b][:],
-                in_=q_listed[:, b * NQ * PACK : (b + 1) * NQ * PACK],
-            )
+            nc.vector.quantize_mx(out=q_codes[b][:].bitcast(FP8X4), scales=q_scales[b][:], in_=q_listed[b][:])
+        quantize_keys(2)
 
         z = [keep.tile([P, N], F32, name=f"z{b}") for b in range(B)]
-        for n in range(2 * B):
+        for n, (i, lo) in enumerate(((0, 0), (0, HALF), (1, 0), (2, 0))):
             b, c0 = n // 2, n % 2 * HALF
             cols = slice(n * HALF, (n + 1) * HALF)
             acc = psum.tile([P, HALF], F32, name=f"scores{n}")
@@ -155,8 +163,8 @@ def tile_attend_bothw_f_kernel(tc, qT, kT, kb, offq, offs, out):
                 out=acc[:],
                 lhsT=q_codes[b][:].bitcast(FP8X4),
                 lhsT_scale=q_scales[b][:],
-                rhs=k_codes[:, cols].bitcast(FP8X4),
-                rhs_scale=k_scales[:, cols],
+                rhs=k_codes[i][:, lo : lo + HALF].bitcast(FP8X4),
+                rhs_scale=k_scales[i][:, lo : lo + HALF],
                 start=True,
                 stop=True,
             )

@@ -60,13 +60,12 @@ def tile_attend_bothw_f_kernel(tc, qT, kT, kb, offq, offs, out):
             raw = keep.tile([P, n * T], F32, name=f"k_raw{t0}")
             nc.sync.dma_start(raw[:], k_rows[:, t0 * T : (t0 + n) * T])
             k_raw.extend(raw[:, i * T : (i + 1) * T] for i in range(n))
+        nc.sync.dma_start(query_list[:], offq)
         q_raw = []
-        for t in range(PACK):
-            raw = keep.tile([P, TQ], F32, name=f"q_raw{t}")
-            nc.sync.dma_start(raw[:], q_rows[:, t * TQ : (t + 1) * TQ])
-            q_raw.append(raw[:])
-            if t == 0:
-                nc.sync.dma_start(query_list[:], offq)
+        for t0, n in ((0, 2), (2, 1), (3, 1)):
+            raw = keep.tile([P, n * TQ], F32, name=f"q_raw{t0}")
+            nc.sync.dma_start(raw[:], q_rows[:, t0 * TQ : (t0 + n) * TQ])
+            q_raw.extend(raw[:, i * TQ : (i + 1) * TQ] for i in range(n))
 
         bias_pool = keep.tile([P, T], F32, name="bias_pool")
         nc.gpsimd.memset(bias_pool[:], 0.0)
@@ -138,7 +137,7 @@ def tile_attend_bothw_f_kernel(tc, qT, kT, kb, offq, offs, out):
             keep.tile([P, NQ * PACK], BF16, name="q_listed1", align_bytes=64),
         ]
         q_words = [q_listed[b][:].rearrange("p (c t) -> p c t", t=PACK) for b in range(B)]
-        q_runs = keep.tile([P, 2, B * NQ], BF16, name="q_runs")
+        q_runs = keep.tile([P, 2, B * NQ], F32, name="q_runs")
         for t in range(2):
             gather(nc, True, q_runs[:, t, :], q_raw[t], query_list[:])
         q_planes = q_runs[:].rearrange("p t c -> p c t")

@@ -21,8 +21,12 @@ P = 128
 PACK = 4
 GROUP = 16
 HALF = N // 2
+PER = T // P
+BANK = 4
 QUERY_BYTES = 2 * NQ * PACK
-KEY_BYTES = 2 * N * PACK
+POOL_AT = B * QUERY_BYTES
+LAST_AT = POOL_AT + 4 * T
+VECTOR_COLS = 352
 
 
 def entries(listed, first, count):
@@ -36,10 +40,6 @@ def gather(nc, on_scalar, out, window, listed):
         nc.vector.tensor_copy(out, window.indirect(listed))
 
 
-def place(copy, out, src):
-    copy(out, src)
-
-
 def tile_attend_bothw_f_kernel(tc, qT, kT, kb, offq, offs, out):
     nc = tc.nc
     with ExitStack() as ctx:
@@ -49,95 +49,82 @@ def tile_attend_bothw_f_kernel(tc, qT, kT, kb, offq, offs, out):
 
         key_list = keep.tile([P, B * N // GROUP], U16, name="key_list")
         query_list = keep.tile([P, B * NQ // GROUP], U16, name="query_list")
-        bias_row = keep.tile([1, T], F32, name="bias_row")
+        bias_cols = keep.tile([P, PER], F32, name="bias_cols")
         k_rows = kT.rearrange("(p t) c -> p (t c)", t=PACK)
         q_rows = qT.rearrange("(p t) c -> p (t c)", t=PACK)
+        k_raw = [keep.tile([P, T], F32, name=f"k_raw{t}") for t in range(PACK - 1)]
+        k_raw.append(placed.tile([P, T], F32, name="k_raw3", align_bytes=64, offset=LAST_AT))
 
-        nc.sync.dma_start(bias_row[:], kb[0:1, :])
+        nc.scalar.dma_start(k_raw[0][:], k_rows[:, 0:T])
+        nc.sync.dma_start(bias_cols[:], kb[0:1, :].rearrange("o (p c) -> p (o c)", c=PER))
         nc.sync.dma_start(key_list[:], offs)
-        k_raw = []
-        for t0, n in ((0, 2), (2, 1), (3, 1)):
-            raw = keep.tile([P, n * T], F32, name=f"k_raw{t0}")
-            nc.sync.dma_start(raw[:], k_rows[:, t0 * T : (t0 + n) * T])
-            k_raw.extend(raw[:, i * T : (i + 1) * T] for i in range(n))
         nc.sync.dma_start(query_list[:], offq)
+        for t in range(1, PACK):
+            nc.sync.dma_start(k_raw[t][:], k_rows[:, t * T : (t + 1) * T])
         q_raw = []
         for t0, n in ((0, 2), (2, 1), (3, 1)):
             raw = keep.tile([P, n * TQ], F32, name=f"q_raw{t0}")
             nc.sync.dma_start(raw[:], q_rows[:, t0 * TQ : (t0 + n) * TQ])
             q_raw.extend(raw[:, i * TQ : (i + 1) * TQ] for i in range(n))
 
-        bias_pool = keep.tile([P, T], F32, name="bias_pool")
-        nc.gpsimd.memset(bias_pool[:], 0.0)
-        nc.vector.tensor_copy(bias_pool[0:1, :], bias_row[:])
-        bias_listed = [keep.tile([P, N], F32, name=f"bias_listed{b}") for b in range(B)]
-        for b in range(B):
-            gather(nc, False, bias_listed[b][:], bias_pool[:], entries(key_list, b * N, N))
-
         ident = keep.tile([P, P], F32, name="ident")
         make_identity(nc, ident[:])
-        blocks = N // P
-        bias_cols = keep.tile([P, B * blocks], F32, name="bias_cols")
-        for b in range(B):
-            turned = psum.tile([P, blocks, P], F32, name=f"turned{b}")
-            for i in range(blocks):
-                nc.tensor.transpose(turned[:, i, :], bias_listed[b][:, i * P : (i + 1) * P], ident[:])
-            nc.scalar.copy(bias_cols[:, b * blocks : (b + 1) * blocks], turned[:, :, 0])
+        bias_pool = placed.tile([P, T], F32, name="bias_pool", align_bytes=64, offset=POOL_AT)
+        in_order = bias_pool[:].rearrange("m (p j i) -> m j p i", j=PER // BANK, i=BANK)
+        for j in range(PER // BANK):
+            spread = psum.tile([P, BANK, P], F32, name=f"spread{j}")
+            for i in range(BANK):
+                c = j * BANK + i
+                nc.tensor.transpose(spread[:, i, :], bias_cols[:, c : c + 1].to_broadcast([P, P]), ident[:])
+            nc.scalar.activation(in_order[:, j], spread[:].rearrange("m i p -> m p i"), ACT.Copy)
         bias = keep.tile([P, B * N], F32, name="bias")
-        for b in range(B):
-            spread = psum.tile([P, blocks, P], F32, name=f"spread{b}")
-            for i in range(blocks):
-                j = b * blocks + i
-                nc.tensor.transpose(spread[:, i, :], bias_cols[:, j : j + 1].to_broadcast([P, P]), ident[:])
-            nc.scalar.copy(bias[:, b * N : (b + 1) * N], spread[:].rearrange("m i p -> m (i p)"))
+        gather(nc, True, bias[:], bias_pool[:], key_list[:])
 
-        k_pairs = [keep.tile([P, 2 * B * N], BF16, name=f"k_pairs{u}") for u in range(2)]
-        k_listed = [
-            placed.tile([P, N * PACK], BF16, name=f"k_listed{b}", align_bytes=64, offset=b * KEY_BYTES)
-            for b in range(B)
+        k_pairs = [
+            keep.tile([P, 2 * B * N], BF16, name="k_pairs0"),
+            placed.tile([P, 2 * B * N], BF16, name="k_pairs1", align_bytes=64, offset=POOL_AT),
         ]
-        by_half = [k_listed[b][:].rearrange("p (i c t) -> p i c t", c=HALF, t=PACK) for b in range(B)]
-        low = k_pairs[0][:].rearrange("p (i t c) -> p i c t", t=2, c=HALF)
-        high = k_pairs[1][:].rearrange("p (t i c) -> p i c t", t=2, c=HALF)
-        low_planes = k_pairs[0][:].rearrange("p (i t c) -> p t i c", t=2, c=HALF)
+        parts = ((0, 2), (2, 1), (3, 1))
+        k_listed = [
+            keep.tile([P, N * PACK], BF16, name="k_listed0", align_bytes=64),
+            placed.tile([P, HALF * PACK], BF16, name="k_listed1", align_bytes=64, offset=0),
+            keep.tile([P, HALF * PACK], BF16, name="k_listed2", align_bytes=64),
+        ]
+        by_half = [k[:].rearrange("p (i c t) -> p i c t", c=HALF, t=PACK) for k in k_listed]
+        low, high = (k_pairs[u][:].rearrange("p (t i c) -> p i c t", t=2, c=HALF) for u in range(2))
         for t in range(2):
-            gather(nc, False, low_planes[:, t], k_raw[t], key_list[:])
-        for b in range(B):
-            place(nc.vector.tensor_copy, by_half[b][:, :, :, 0:2], low[:, 2 * b : 2 * b + 2])
-        gather(nc, True, k_pairs[1][:, 0 : B * N], k_raw[2], key_list[:])
+            gather(nc, False, k_pairs[0][:, t * B * N : (t + 1) * B * N], k_raw[t][:], key_list[:])
+        for i, (h0, n) in enumerate(parts):
+            nc.vector.tensor_copy(by_half[i][:, :, :, 0:2], low[:, h0 : h0 + n])
+        gather(nc, True, k_pairs[1][:, 0 : B * N], k_raw[2][:], key_list[:])
         for i in range(2):
             run = k_pairs[1][:, B * N + i * HALF : B * N + (i + 1) * HALF]
-            gather(nc, False, run, k_raw[3], entries(key_list, i * HALF, HALF))
-        gather(nc, True, k_pairs[1][:, (B + 1) * N :], k_raw[3], entries(key_list, N, N))
+            gather(nc, False, run, k_raw[3][:], entries(key_list, i * HALF, HALF))
+        gather(nc, True, k_pairs[1][:, (B + 1) * N :], k_raw[3][:], entries(key_list, N, N))
         for i in range(2):
-            place(nc.vector.tensor_copy, by_half[0][:, i : i + 1, :, 2:4], high[:, i : i + 1])
-        place(nc.vector.tensor_copy, by_half[1][:, :, :, 2:4], high[:, 2:4])
+            nc.vector.tensor_copy(by_half[0][:, i : i + 1, :, 2:4], high[:, i : i + 1])
+        for i in range(1, 3):
+            nc.vector.tensor_copy(by_half[i][:, :, :, 2:4], high[:, i + 1 : i + 2])
 
-        parts = ((0, 0, N), (1, 0, HALF), (1, HALF, HALF))
-        k_codes = [keep.tile([P, w], U32, name=f"k_codes{i}", align_bytes=64) for i, (b, c0, w) in enumerate(parts)]
+        k_codes = [keep.tile([P, n * HALF], U32, name=f"k_codes{h0}", align_bytes=64) for h0, n in parts]
         k_scales = [
             keep.tile([P, N], U8, name="k_scales0", align_bytes=64),
             keep.tile([P, HALF], U8, name="k_scales1", align_bytes=64),
-            placed.tile([P, HALF], U8, name="k_scales2", align_bytes=64, offset=B * KEY_BYTES),
+            placed.tile([P, HALF], U8, name="k_scales2", align_bytes=64, offset=0),
         ]
 
         def quantize_keys(i):
-            b, c0, w = parts[i]
-            nc.vector.quantize_mx(
-                out=k_codes[i][:].bitcast(FP8X4),
-                scales=k_scales[i][:],
-                in_=k_listed[b][:, c0 * PACK : (c0 + w) * PACK],
-            )
+            nc.vector.quantize_mx(out=k_codes[i][:].bitcast(FP8X4), scales=k_scales[i][:], in_=k_listed[i][:])
 
         quantize_keys(0)
         quantize_keys(1)
 
         q_listed = [
-            placed.tile([P, NQ * PACK], BF16, name="q_listed0", align_bytes=64, offset=B * KEY_BYTES),
-            keep.tile([P, NQ * PACK], BF16, name="q_listed1", align_bytes=64),
+            placed.tile([P, NQ * PACK], BF16, name=f"q_listed{b}", align_bytes=64, offset=b * QUERY_BYTES)
+            for b in range(B)
         ]
         q_words = [q_listed[b][:].rearrange("p (c t) -> p c t", t=PACK) for b in range(B)]
-        q_runs = keep.tile([P, 2, B * NQ], F32, name="q_runs")
+        q_runs = placed.tile([P, 2, B * NQ], F32, name="q_runs", align_bytes=64, offset=LAST_AT)
         for t in range(2):
             gather(nc, True, q_runs[:, t, :], q_raw[t], query_list[:])
         q_planes = q_runs[:].rearrange("p t c -> p c t")
@@ -174,14 +161,16 @@ def tile_attend_bothw_f_kernel(tc, qT, kT, kb, offq, offs, out):
             nm = keep.tile([P, 1], F32, name=f"neg_max{b}")
             nc.vector.tensor_reduce(nm[:], z[b][:], AX.X, ALU.max, negate=True)
             neg_max.append(nm)
+        e = [keep.tile([P, N], F32, name=f"e{b}") for b in range(B)]
+        total = [keep.tile([P, 1], F32, name=f"total{b}") for b in range(B)]
         for b in range(B):
-            e = keep.tile([P, N], F32, name=f"e{b}")
-            total = keep.tile([P, 1], F32, name=f"total{b}")
-            nc.scalar.activation(e[:], z[b][:], ACT.Exp, bias=neg_max[b][:], scale=1.0, accum_out=total[:])
+            nc.scalar.activation(e[b][:], z[b][:], ACT.Exp, bias=neg_max[b][:], scale=1.0, accum_out=total[b][:])
+
+        for b, cut in enumerate((HALF, VECTOR_COLS)):
             inverse = keep.tile([P, 1], F32, name=f"inverse{b}")
-            nc.vector.reciprocal(inverse[:], total[:])
-            cut = N // 4 if b == 0 else HALF
-            for i, cols in enumerate((slice(0, cut), slice(cut, N))):
-                y = keep.tile([P, cols.stop - cols.start], F32, name=f"y{b}_{i}")
-                nc.vector.tensor_scalar(y[:], e[:, cols], inverse[:], None, ALU.mult)
-                nc.sync.dma_start(out[b][:, cols], y[:])
+            nc.vector.reciprocal(inverse[:], total[b][:])
+            y = keep.tile([P, N], F32, name=f"y{b}")
+            nc.vector.tensor_scalar(y[:, :cut], e[b][:, :cut], inverse[:], None, ALU.mult)
+            nc.scalar.activation(y[:, cut:], e[b][:, cut:], ACT.Copy, scale=inverse[:])
+            for cols in (slice(0, cut), slice(cut, N)) if b == 0 else (slice(0, N),):
+                nc.sync.dma_start(out[b][:, cols], y[:, cols])

@@ -26,7 +26,6 @@ BANK = 4
 QUERY_BYTES = 2 * NQ * PACK
 POOL_AT = B * QUERY_BYTES
 LAST_AT = POOL_AT + 4 * T
-VECTOR_COLS = 352
 
 
 def entries(listed, first, count):
@@ -166,11 +165,10 @@ def tile_attend_bothw_f_kernel(tc, qT, kT, kb, offq, offs, out):
         for b in range(B):
             nc.scalar.activation(e[b][:], z[b][:], ACT.Exp, bias=neg_max[b][:], scale=1.0, accum_out=total[b][:])
 
-        for b, cut in enumerate((HALF, VECTOR_COLS)):
+        for b, cut in enumerate((N // 4, HALF)):
             inverse = keep.tile([P, 1], F32, name=f"inverse{b}")
             nc.vector.reciprocal(inverse[:], total[b][:])
-            y = keep.tile([P, N], F32, name=f"y{b}")
-            nc.vector.tensor_scalar(y[:, :cut], e[b][:, :cut], inverse[:], None, ALU.mult)
-            nc.scalar.activation(y[:, cut:], e[b][:, cut:], ACT.Copy, scale=inverse[:])
-            for cols in (slice(0, cut), slice(cut, N)) if b == 0 else (slice(0, N),):
-                nc.sync.dma_start(out[b][:, cols], y[:, cols])
+            for i, cols in enumerate((slice(0, cut), slice(cut, N))):
+                y = keep.tile([P, cols.stop - cols.start], F32, name=f"y{b}_{i}")
+                nc.vector.tensor_scalar(y[:], e[b][:, cols], inverse[:], None, ALU.mult)
+                nc.sync.dma_start(out[b][:, cols], y[:])

@@ -54,10 +54,11 @@ def tile_attend_bothw_f_kernel(tc, qT, kT, kb, offq, offs, out):
         k_raw = [keep.tile([P, T], F32, name=f"k_raw{t}") for t in range(PACK - 1)]
         k_raw.append(placed.tile([P, T], F32, name="k_raw3", align_bytes=64, offset=LAST_AT))
 
-        nc.scalar.dma_start(k_raw[0][:], k_rows[:, 0:T])
+        nc.scalar.dma_start(k_raw[0][:, : T // 2], k_rows[:, : T // 2])
         nc.sync.dma_start(bias_cols[:], kb[0:1, :].rearrange("o (p c) -> p (o c)", c=PER))
         nc.sync.dma_start(key_list[:], offs)
         nc.sync.dma_start(query_list[:], offq)
+        nc.sync.dma_start(k_raw[0][:, T // 2 :], k_rows[:, T // 2 : T])
         for t in range(1, PACK):
             nc.sync.dma_start(k_raw[t][:], k_rows[:, t * T : (t + 1) * T])
         q_raw = []
@@ -95,15 +96,14 @@ def tile_attend_bothw_f_kernel(tc, qT, kT, kb, offq, offs, out):
             gather(nc, False, k_pairs[0][:, t * B * N : (t + 1) * B * N], k_raw[t][:], key_list[:])
         for i, (h0, n) in enumerate(parts):
             nc.vector.tensor_copy(by_half[i][:, :, :, 0:2], low[:, h0 : h0 + n])
-        gather(nc, True, k_pairs[1][:, 0 : B * N], k_raw[2][:], key_list[:])
-        for i in range(2):
+        for b in range(B):
+            gather(nc, b == 1, k_pairs[1][:, b * N : (b + 1) * N], k_raw[2][:], entries(key_list, b * N, N))
+        for i in range(2 * B):
             run = k_pairs[1][:, B * N + i * HALF : B * N + (i + 1) * HALF]
-            gather(nc, False, run, k_raw[3][:], entries(key_list, i * HALF, HALF))
-        gather(nc, True, k_pairs[1][:, (B + 1) * N :], k_raw[3][:], entries(key_list, N, N))
+            gather(nc, i > 0, run, k_raw[3][:], entries(key_list, i * HALF, HALF))
         for i in range(2):
             nc.vector.tensor_copy(by_half[0][:, i : i + 1, :, 2:4], high[:, i : i + 1])
-        for i in range(1, 3):
-            nc.vector.tensor_copy(by_half[i][:, :, :, 2:4], high[:, i + 1 : i + 2])
+        nc.vector.tensor_copy(by_half[1][:, :, :, 2:4], high[:, 2:3])
 
         k_codes = [keep.tile([P, n * HALF], U32, name=f"k_codes{h0}", align_bytes=64) for h0, n in parts]
         k_scales = [
@@ -117,6 +117,7 @@ def tile_attend_bothw_f_kernel(tc, qT, kT, kb, offq, offs, out):
 
         quantize_keys(0)
         quantize_keys(1)
+        nc.vector.tensor_copy(by_half[2][:, :, :, 2:4], high[:, 3:4])
 
         q_listed = [
             placed.tile([P, NQ * PACK], BF16, name=f"q_listed{b}", align_bytes=64, offset=b * QUERY_BYTES)

@@ -25,7 +25,9 @@ PER = T // P
 BANK = 4
 QUERY_BYTES = 2 * NQ * PACK
 POOL_AT = B * QUERY_BYTES
-LAST_AT = POOL_AT + 4 * T
+EARLY_AT = POOL_AT + 2 * T
+THIRD_AT = EARLY_AT + 4 * 2 * TQ
+LAST_AT = THIRD_AT + 4 * T
 
 
 def entries(listed, first, count):
@@ -48,24 +50,18 @@ def tile_attend_bothw_f_kernel(tc, qT, kT, kb, offq, offs, out):
 
         key_list = keep.tile([P, B * N // GROUP], U16, name="key_list")
         query_list = keep.tile([P, B * NQ // GROUP], U16, name="query_list")
-        bias_cols = keep.tile([P, PER], F32, name="bias_cols")
+        bias_cols = placed.tile([P, PER], F32, name="bias_cols", align_bytes=64, offset=LAST_AT)
         k_rows = kT.rearrange("(p t) c -> p (t c)", t=PACK)
         q_rows = qT.rearrange("(p t) c -> p (t c)", t=PACK)
-        k_raw = [keep.tile([P, T], F32, name=f"k_raw{t}") for t in range(PACK - 1)]
-        k_raw.append(placed.tile([P, T], F32, name="k_raw3", align_bytes=64, offset=LAST_AT))
+        k_raw = [keep.tile([P, T], F32, name=f"k_raw{t}") for t in range(2)]
+        for t, at in ((2, THIRD_AT), (3, LAST_AT)):
+            k_raw.append(placed.tile([P, T], F32, name=f"k_raw{t}", align_bytes=64, offset=at))
 
-        nc.scalar.dma_start(k_raw[0][:, : T // 2], k_rows[:, : T // 2])
         nc.sync.dma_start(bias_cols[:], kb[0:1, :].rearrange("o (p c) -> p (o c)", c=PER))
         nc.sync.dma_start(key_list[:], offs)
         nc.sync.dma_start(query_list[:], offq)
-        nc.sync.dma_start(k_raw[0][:, T // 2 :], k_rows[:, T // 2 : T])
-        for t in range(1, PACK):
-            nc.sync.dma_start(k_raw[t][:], k_rows[:, t * T : (t + 1) * T])
-        q_raw = []
-        for t0, n in ((0, 2), (2, 1), (3, 1)):
-            raw = keep.tile([P, n * TQ], F32, name=f"q_raw{t0}")
-            nc.sync.dma_start(raw[:], q_rows[:, t0 * TQ : (t0 + n) * TQ])
-            q_raw.extend(raw[:, i * TQ : (i + 1) * TQ] for i in range(n))
+        for t in range(PACK - 1):
+            nc.scalar.dma_start(k_raw[t][:], k_rows[:, t * T : (t + 1) * T])
 
         ident = keep.tile([P, P], F32, name="ident")
         make_identity(nc, ident[:])
@@ -77,8 +73,12 @@ def tile_attend_bothw_f_kernel(tc, qT, kT, kb, offq, offs, out):
                 c = j * BANK + i
                 nc.tensor.transpose(spread[:, i, :], bias_cols[:, c : c + 1].to_broadcast([P, P]), ident[:])
             nc.scalar.activation(in_order[:, j], spread[:].rearrange("m i p -> m p i"), ACT.Copy)
+        nc.sync.dma_start(k_raw[3][:], k_rows[:, 3 * T :])
         bias = keep.tile([P, B * N], F32, name="bias")
         gather(nc, True, bias[:], bias_pool[:], key_list[:])
+        q_early = placed.tile([P, 2 * TQ], F32, name="q_early", align_bytes=64, offset=EARLY_AT)
+        nc.scalar.dma_start(q_early[:], q_rows[:, : 2 * TQ])
+        q_raw = [q_early[:, :TQ], q_early[:, TQ:]]
 
         k_pairs = [
             keep.tile([P, 2 * B * N], BF16, name="k_pairs0"),
@@ -98,6 +98,10 @@ def tile_attend_bothw_f_kernel(tc, qT, kT, kb, offq, offs, out):
             nc.vector.tensor_copy(by_half[i][:, :, :, 0:2], low[:, h0 : h0 + n])
         for b in range(B):
             gather(nc, b == 1, k_pairs[1][:, b * N : (b + 1) * N], k_raw[2][:], entries(key_list, b * N, N))
+        for t in range(2, PACK):
+            late = placed.tile([P, TQ], F32, name=f"q_raw{t}", align_bytes=64, offset=THIRD_AT + (t - 2) * 4 * TQ)
+            nc.sync.dma_start(late[:], q_rows[:, t * TQ : (t + 1) * TQ])
+            q_raw.append(late[:])
         for i in range(2 * B):
             run = k_pairs[1][:, B * N + i * HALF : B * N + (i + 1) * HALF]
             gather(nc, i > 0, run, k_raw[3][:], entries(key_list, i * HALF, HALF))

@@ -25,9 +25,10 @@ PER = T // P
 BANK = 4
 QUERY_BYTES = 2 * NQ * PACK
 POOL_AT = B * QUERY_BYTES
-EARLY_AT = POOL_AT + 2 * T
-THIRD_AT = EARLY_AT + 4 * 2 * TQ
-LAST_AT = THIRD_AT + 4 * T
+LAST_AT = POOL_AT + 4 * T
+FIRST_AT = LAST_AT + 2 * T
+EARLY_AT = LAST_AT + 4 * T
+SECOND_AT = EARLY_AT + 4 * 2 * TQ
 
 
 def entries(listed, first, count):
@@ -50,12 +51,15 @@ def tile_attend_bothw_f_kernel(tc, qT, kT, kb, offq, offs, out):
 
         key_list = keep.tile([P, B * N // GROUP], U16, name="key_list")
         query_list = keep.tile([P, B * NQ // GROUP], U16, name="query_list")
-        bias_cols = placed.tile([P, PER], F32, name="bias_cols", align_bytes=64, offset=LAST_AT)
+        bias_cols = keep.tile([P, PER], F32, name="bias_cols")
         k_rows = kT.rearrange("(p t) c -> p (t c)", t=PACK)
         q_rows = qT.rearrange("(p t) c -> p (t c)", t=PACK)
-        k_raw = [keep.tile([P, T], F32, name=f"k_raw{t}") for t in range(2)]
-        for t, at in ((2, THIRD_AT), (3, LAST_AT)):
-            k_raw.append(placed.tile([P, T], F32, name=f"k_raw{t}", align_bytes=64, offset=at))
+        k_raw = [
+            placed.tile([P, T], F32, name="k_raw0", align_bytes=64, offset=FIRST_AT),
+            placed.tile([P, T], F32, name="k_raw1", align_bytes=64, offset=SECOND_AT),
+            keep.tile([P, T], F32, name="k_raw2"),
+            placed.tile([P, T], F32, name="k_raw3", align_bytes=64, offset=LAST_AT),
+        ]
 
         nc.sync.dma_start(bias_cols[:], kb[0:1, :].rearrange("o (p c) -> p (o c)", c=PER))
         nc.sync.dma_start(key_list[:], offs)
@@ -73,12 +77,8 @@ def tile_attend_bothw_f_kernel(tc, qT, kT, kb, offq, offs, out):
                 c = j * BANK + i
                 nc.tensor.transpose(spread[:, i, :], bias_cols[:, c : c + 1].to_broadcast([P, P]), ident[:])
             nc.scalar.activation(in_order[:, j], spread[:].rearrange("m i p -> m p i"), ACT.Copy)
-        nc.sync.dma_start(k_raw[3][:], k_rows[:, 3 * T :])
         bias = keep.tile([P, B * N], F32, name="bias")
         gather(nc, True, bias[:], bias_pool[:], key_list[:])
-        q_early = placed.tile([P, 2 * TQ], F32, name="q_early", align_bytes=64, offset=EARLY_AT)
-        nc.scalar.dma_start(q_early[:], q_rows[:, : 2 * TQ])
-        q_raw = [q_early[:, :TQ], q_early[:, TQ:]]
 
         k_pairs = [
             keep.tile([P, 2 * B * N], BF16, name="k_pairs0"),
@@ -94,14 +94,16 @@ def tile_attend_bothw_f_kernel(tc, qT, kT, kb, offq, offs, out):
         low, high = (k_pairs[u][:].rearrange("p (t i c) -> p i c t", t=2, c=HALF) for u in range(2))
         for t in range(2):
             gather(nc, False, k_pairs[0][:, t * B * N : (t + 1) * B * N], k_raw[t][:], key_list[:])
+        nc.sync.dma_start(k_raw[3][:], k_rows[:, 3 * T :])
+        q_raw = []
+        for t0, n, at in ((0, 2, EARLY_AT), (2, 1, SECOND_AT), (3, 1, SECOND_AT + 4 * TQ)):
+            raw = placed.tile([P, n * TQ], F32, name=f"q_raw{t0}", align_bytes=64, offset=at)
+            nc.sync.dma_start(raw[:], q_rows[:, t0 * TQ : (t0 + n) * TQ])
+            q_raw.extend(raw[:, i * TQ : (i + 1) * TQ] for i in range(n))
         for i, (h0, n) in enumerate(parts):
             nc.vector.tensor_copy(by_half[i][:, :, :, 0:2], low[:, h0 : h0 + n])
         for b in range(B):
             gather(nc, b == 1, k_pairs[1][:, b * N : (b + 1) * N], k_raw[2][:], entries(key_list, b * N, N))
-        for t in range(2, PACK):
-            late = placed.tile([P, TQ], F32, name=f"q_raw{t}", align_bytes=64, offset=THIRD_AT + (t - 2) * 4 * TQ)
-            nc.sync.dma_start(late[:], q_rows[:, t * TQ : (t + 1) * TQ])
-            q_raw.append(late[:])
         for i in range(2 * B):
             run = k_pairs[1][:, B * N + i * HALF : B * N + (i + 1) * HALF]
             gather(nc, i > 0, run, k_raw[3][:], entries(key_list, i * HALF, HALF))

@@ -24,11 +24,9 @@ HALF = N // 2
 PER = T // P
 BANK = 4
 QUERY_BYTES = 2 * NQ * PACK
-POOL_AT = B * QUERY_BYTES
-LAST_AT = POOL_AT + 4 * T
-FIRST_AT = LAST_AT + 2 * T
-EARLY_AT = LAST_AT + 4 * T
-SECOND_AT = EARLY_AT + 4 * 2 * TQ
+POOL_AT = 2 * N * PACK
+EARLY_AT = POOL_AT + 4 * T
+LATE_AT = EARLY_AT + 4 * 2 * T
 
 
 def entries(listed, first, count):
@@ -54,18 +52,15 @@ def tile_attend_bothw_f_kernel(tc, qT, kT, kb, offq, offs, out):
         bias_cols = keep.tile([P, PER], F32, name="bias_cols")
         k_rows = kT.rearrange("(p t) c -> p (t c)", t=PACK)
         q_rows = qT.rearrange("(p t) c -> p (t c)", t=PACK)
-        k_raw = [
-            placed.tile([P, T], F32, name="k_raw0", align_bytes=64, offset=FIRST_AT),
-            placed.tile([P, T], F32, name="k_raw1", align_bytes=64, offset=SECOND_AT),
-            keep.tile([P, T], F32, name="k_raw2"),
-            placed.tile([P, T], F32, name="k_raw3", align_bytes=64, offset=LAST_AT),
-        ]
+        k_raw = []
 
         nc.sync.dma_start(bias_cols[:], kb[0:1, :].rearrange("o (p c) -> p (o c)", c=PER))
         nc.sync.dma_start(key_list[:], offs)
         nc.sync.dma_start(query_list[:], offq)
-        for t in range(PACK - 1):
-            nc.scalar.dma_start(k_raw[t][:], k_rows[:, t * T : (t + 1) * T])
+        for u, at in enumerate((EARLY_AT, LATE_AT)):
+            raw = placed.tile([P, 2 * T], F32, name=f"k_raw{u}", align_bytes=64, offset=at)
+            nc.scalar.dma_start(raw[:], k_rows[:, 2 * u * T : 2 * (u + 1) * T])
+            k_raw.extend(raw[:, i * T : (i + 1) * T] for i in range(2))
 
         ident = keep.tile([P, P], F32, name="ident")
         make_identity(nc, ident[:])
@@ -80,36 +75,36 @@ def tile_attend_bothw_f_kernel(tc, qT, kT, kb, offq, offs, out):
         bias = keep.tile([P, B * N], F32, name="bias")
         gather(nc, True, bias[:], bias_pool[:], key_list[:])
 
-        k_pairs = [
-            keep.tile([P, 2 * B * N], BF16, name="k_pairs0"),
-            placed.tile([P, 2 * B * N], BF16, name="k_pairs1", align_bytes=64, offset=POOL_AT),
-        ]
         parts = ((0, 2), (2, 1), (3, 1))
         k_listed = [
-            keep.tile([P, N * PACK], BF16, name="k_listed0", align_bytes=64),
-            placed.tile([P, HALF * PACK], BF16, name="k_listed1", align_bytes=64, offset=0),
+            placed.tile([P, N * PACK], BF16, name="k_listed0", align_bytes=64, offset=0),
+            keep.tile([P, HALF * PACK], BF16, name="k_listed1", align_bytes=64),
             keep.tile([P, HALF * PACK], BF16, name="k_listed2", align_bytes=64),
         ]
         by_half = [k[:].rearrange("p (i c t) -> p i c t", c=HALF, t=PACK) for k in k_listed]
-        low, high = (k_pairs[u][:].rearrange("p (t i c) -> p i c t", t=2, c=HALF) for u in range(2))
+        early = keep.tile([P, 2 * B * N], F32, name="early_runs")
         for t in range(2):
-            gather(nc, False, k_pairs[0][:, t * B * N : (t + 1) * B * N], k_raw[t][:], key_list[:])
-        nc.sync.dma_start(k_raw[3][:], k_rows[:, 3 * T :])
+            gather(nc, False, early[:, t * B * N : (t + 1) * B * N], k_raw[t], key_list[:])
         q_raw = []
-        for t0, n, at in ((0, 2, EARLY_AT), (2, 1, SECOND_AT), (3, 1, SECOND_AT + 4 * TQ)):
-            raw = placed.tile([P, n * TQ], F32, name=f"q_raw{t0}", align_bytes=64, offset=at)
+        for t0, n in ((0, 2), (2, 1), (3, 1)):
+            raw = placed.tile([P, n * TQ], F32, name=f"q_raw{t0}", align_bytes=64, offset=EARLY_AT + 4 * t0 * TQ)
             nc.sync.dma_start(raw[:], q_rows[:, t0 * TQ : (t0 + n) * TQ])
             q_raw.extend(raw[:, i * TQ : (i + 1) * TQ] for i in range(n))
+        low = early[:].rearrange("p (t i c) -> p i c t", t=2, c=HALF)
         for i, (h0, n) in enumerate(parts):
             nc.vector.tensor_copy(by_half[i][:, :, :, 0:2], low[:, h0 : h0 + n])
-        for b in range(B):
-            gather(nc, b == 1, k_pairs[1][:, b * N : (b + 1) * N], k_raw[2][:], entries(key_list, b * N, N))
+
+        late = [
+            placed.tile([P, 2, HALF], F32, name=f"late_runs{i}", align_bytes=64, offset=POOL_AT + i * 8 * HALF)
+            for i in range(2 * B)
+        ]
         for i in range(2 * B):
-            run = k_pairs[1][:, B * N + i * HALF : B * N + (i + 1) * HALF]
-            gather(nc, i > 0, run, k_raw[3][:], entries(key_list, i * HALF, HALF))
-        for i in range(2):
-            nc.vector.tensor_copy(by_half[0][:, i : i + 1, :, 2:4], high[:, i : i + 1])
-        nc.vector.tensor_copy(by_half[1][:, :, :, 2:4], high[:, 2:3])
+            for t in range(2):
+                gather(nc, 2 * i + t > 2, late[i][:, t, :], k_raw[2 + t], entries(key_list, i * HALF, HALF))
+        halves = (by_half[0][:, 0], by_half[0][:, 1], by_half[1][:, 0], by_half[2][:, 0])
+
+        def place_late(i):
+            nc.vector.tensor_copy(halves[i][:, :, 2:4], late[i][:].rearrange("p t c -> p c t"))
 
         k_codes = [keep.tile([P, n * HALF], U32, name=f"k_codes{h0}", align_bytes=64) for h0, n in parts]
         k_scales = [
@@ -121,35 +116,44 @@ def tile_attend_bothw_f_kernel(tc, qT, kT, kb, offq, offs, out):
         def quantize_keys(i):
             nc.vector.quantize_mx(out=k_codes[i][:].bitcast(FP8X4), scales=k_scales[i][:], in_=k_listed[i][:])
 
+        for i in range(3):
+            place_late(i)
         quantize_keys(0)
         quantize_keys(1)
-        nc.vector.tensor_copy(by_half[2][:, :, :, 2:4], high[:, 3:4])
+        place_late(3)
 
         q_listed = [
             placed.tile([P, NQ * PACK], BF16, name=f"q_listed{b}", align_bytes=64, offset=b * QUERY_BYTES)
             for b in range(B)
         ]
         q_words = [q_listed[b][:].rearrange("p (c t) -> p c t", t=PACK) for b in range(B)]
-        q_runs = placed.tile([P, 2, B * NQ], F32, name="q_runs", align_bytes=64, offset=LAST_AT)
-        for t in range(2):
-            gather(nc, True, q_runs[:, t, :], q_raw[t], query_list[:])
-        q_planes = q_runs[:].rearrange("p t c -> p c t")
         for b in range(B):
-            nc.scalar.copy(q_words[b][:, :, 0:2], q_planes[:, b * NQ : (b + 1) * NQ, :])
-        for t in range(2, PACK):
-            for b in range(B):
-                gather(nc, False, q_words[b][:, :, t], q_raw[t], entries(query_list, b * NQ, NQ))
-
+            runs = placed.tile([P, 2, NQ], F32, name=f"q_runs{b}", align_bytes=64, offset=LATE_AT + b * 8 * NQ)
+            for t in range(2):
+                gather(nc, True, runs[:, t, :], q_raw[t], entries(query_list, b * NQ, NQ))
+            nc.scalar.copy(q_words[b][:, :, 0:2], runs[:].rearrange("p t c -> p c t"))
         q_codes = [keep.tile([P, NQ], U32, name=f"q_codes{b}", align_bytes=64) for b in range(B)]
         q_scales = [keep.tile([P, NQ], U8, name=f"q_scales{b}", align_bytes=64) for b in range(B)]
-        for b in range(B):
-            nc.vector.quantize_mx(out=q_codes[b][:].bitcast(FP8X4), scales=q_scales[b][:], in_=q_listed[b][:])
-        quantize_keys(2)
 
-        z = [keep.tile([P, N], F32, name=f"z{b}") for b in range(B)]
-        for n, (i, lo) in enumerate(((0, 0), (0, HALF), (1, 0), (2, 0))):
+        def gather_queries(t, b):
+            gather(nc, False, q_words[b][:, :, t], q_raw[t], entries(query_list, b * NQ, NQ))
+
+        def quantize_queries(b):
+            nc.vector.quantize_mx(out=q_codes[b][:].bitcast(FP8X4), scales=q_scales[b][:], in_=q_listed[b][:])
+
+        for b in range(B):
+            gather_queries(2, b)
+        gather_queries(3, 0)
+        quantize_queries(0)
+        gather_queries(3, 1)
+        quantize_keys(2)
+        quantize_queries(1)
+
+        z = [keep.tile([P, N + 1 - b], F32, name=f"z{b}") for b in range(B)]
+        neg_max = [keep.tile([P, 1], F32, name=f"neg_max{b}") for b in range(B)]
+
+        def score(n, i, lo):
             b, c0 = n // 2, n % 2 * HALF
-            cols = slice(n * HALF, (n + 1) * HALF)
             acc = psum.tile([P, HALF], F32, name=f"scores{n}")
             nc.tensor.matmul_mx(
                 out=acc[:],
@@ -160,17 +164,22 @@ def tile_attend_bothw_f_kernel(tc, qT, kT, kb, offq, offs, out):
                 start=True,
                 stop=True,
             )
-            nc.vector.tensor_tensor(z[b][:, c0 : c0 + HALF], acc[:], bias[:, cols], ALU.add)
+            nc.vector.tensor_tensor(z[b][:, c0 : c0 + HALF], acc[:], bias[:, n * HALF : (n + 1) * HALF], ALU.add)
 
-        neg_max = []
-        for b in range(B):
-            nm = keep.tile([P, 1], F32, name=f"neg_max{b}")
-            nc.vector.tensor_reduce(nm[:], z[b][:], AX.X, ALU.max, negate=True)
-            neg_max.append(nm)
+        score(0, 0, 0)
+        score(1, 0, HALF)
+        nc.vector.tensor_reduce(z[0][:, N:], z[0][:, :HALF], AX.X, ALU.max)
+        score(2, 1, 0)
+        score(3, 2, 0)
+        nc.vector.tensor_reduce(neg_max[0][:], z[0][:, HALF:], AX.X, ALU.max, negate=True)
+        nc.vector.tensor_reduce(neg_max[1][:], z[1][:], AX.X, ALU.max, negate=True)
+
         e = [keep.tile([P, N], F32, name=f"e{b}") for b in range(B)]
         total = [keep.tile([P, 1], F32, name=f"total{b}") for b in range(B)]
         for b in range(B):
-            nc.scalar.activation(e[b][:], z[b][:], ACT.Exp, bias=neg_max[b][:], scale=1.0, accum_out=total[b][:])
+            nc.scalar.activation(
+                e[b][:], z[b][:, :N], ACT.Exp, bias=neg_max[b][:], scale=1.0, accum_out=total[b][:]
+            )
 
         for b, cut in enumerate((N // 4, HALF)):
             inverse = keep.tile([P, 1], F32, name=f"inverse{b}")

@@ -135,17 +135,15 @@ def tile_attend_bothw_f_kernel(tc, qT, kT, kb, offq, offs, out):
         q_codes = [keep.tile([P, NQ], U32, name=f"q_codes{b}", align_bytes=64) for b in range(B)]
         q_scales = [keep.tile([P, NQ], U8, name=f"q_scales{b}", align_bytes=64) for b in range(B)]
 
-        def gather_queries(t, b):
-            gather(nc, False, q_words[b][:, :, t], q_raw[t], entries(query_list, b * NQ, NQ))
-
         def quantize_queries(b):
             nc.vector.quantize_mx(out=q_codes[b][:].bitcast(FP8X4), scales=q_scales[b][:], in_=q_listed[b][:])
 
-        for b in range(B):
-            gather_queries(2, b)
-        gather_queries(3, 0)
+        last_runs = placed.tile([P, 2, NQ], BF16, name="last_runs", align_bytes=64, offset=B * QUERY_BYTES)
+        for t in range(2, PACK):
+            gather(nc, False, q_words[0][:, :, t], q_raw[t], entries(query_list, 0, NQ))
+            gather(nc, False, last_runs[:, t - 2, :], q_raw[t], entries(query_list, NQ, NQ))
         quantize_queries(0)
-        gather_queries(3, 1)
+        nc.vector.tensor_copy(q_words[1][:, :, 2:4], last_runs[:].rearrange("p t c -> p c t"))
         quantize_keys(2)
         quantize_queries(1)
 

@@ -81,18 +81,18 @@ def tile_attend_bothw_f_kernel(tc, qT, kT, kb, offq, offs, out):
             keep.tile([P, HALF * PACK], BF16, name="k_listed1", align_bytes=64),
             keep.tile([P, HALF * PACK], BF16, name="k_listed2", align_bytes=64),
         ]
-        by_half = [k[:].rearrange("p (i c t) -> p i c t", c=HALF, t=PACK) for k in k_listed]
+        by_half = [k[:].rearrange("p (i c w h) -> p i c w h", c=HALF, w=2, h=2) for k in k_listed]
         early = keep.tile([P, 2 * B * N], F32, name="early_runs")
         for t in range(2):
             gather(nc, False, early[:, t * B * N : (t + 1) * B * N], k_raw[t], key_list[:])
         q_raw = []
-        for t0, n in ((0, 2), (2, 1), (3, 1)):
-            raw = placed.tile([P, n * TQ], F32, name=f"q_raw{t0}", align_bytes=64, offset=EARLY_AT + 4 * t0 * TQ)
-            nc.sync.dma_start(raw[:], q_rows[:, t0 * TQ : (t0 + n) * TQ])
-            q_raw.extend(raw[:, i * TQ : (i + 1) * TQ] for i in range(n))
+        for h in range(2):
+            raw = placed.tile([P, 2 * TQ], F32, name=f"q_raw{h}", align_bytes=64, offset=EARLY_AT + 8 * h * TQ)
+            nc.sync.dma_start(raw[:], q_rows[:, 2 * h * TQ : 2 * (h + 1) * TQ])
+            q_raw.append(raw)
         low = early[:].rearrange("p (t i c) -> p i c t", t=2, c=HALF)
         for i, (h0, n) in enumerate(parts):
-            nc.vector.tensor_copy(by_half[i][:, :, :, 0:2], low[:, h0 : h0 + n])
+            nc.vector.tensor_copy(by_half[i][:, :, :, :, 0], low[:, h0 : h0 + n])
 
         late = [
             placed.tile([P, 2, HALF], F32, name=f"late_runs{i}", align_bytes=64, offset=POOL_AT + i * 8 * HALF)
@@ -100,11 +100,11 @@ def tile_attend_bothw_f_kernel(tc, qT, kT, kb, offq, offs, out):
         ]
         for i in range(2 * B):
             for t in range(2):
-                gather(nc, 2 * i + t > 2, late[i][:, t, :], k_raw[2 + t], entries(key_list, i * HALF, HALF))
+                gather(nc, i > 0, late[i][:, t, :], k_raw[2 + t], entries(key_list, i * HALF, HALF))
         halves = (by_half[0][:, 0], by_half[0][:, 1], by_half[1][:, 0], by_half[2][:, 0])
 
         def place_late(i):
-            nc.vector.tensor_copy(halves[i][:, :, 2:4], late[i][:].rearrange("p t c -> p c t"))
+            nc.vector.tensor_copy(halves[i][:, :, :, 1], late[i][:].rearrange("p t c -> p c t"))
 
         k_codes = [keep.tile([P, n * HALF], U32, name=f"k_codes{h0}", align_bytes=64) for h0, n in parts]
         k_scales = [
@@ -127,21 +127,18 @@ def tile_attend_bothw_f_kernel(tc, qT, kT, kb, offq, offs, out):
             for b in range(B)
         ]
         q_words = [q_listed[b][:].rearrange("p (c t) -> p c t", t=PACK) for b in range(B)]
-        for b in range(B):
-            runs = placed.tile([P, 2, NQ], F32, name=f"q_runs{b}", align_bytes=64, offset=LATE_AT + b * 8 * NQ)
-            for t in range(2):
-                gather(nc, True, runs[:, t, :], q_raw[t], entries(query_list, b * NQ, NQ))
-            nc.scalar.copy(q_words[b][:, :, 0:2], runs[:].rearrange("p t c -> p c t"))
         q_codes = [keep.tile([P, NQ], U32, name=f"q_codes{b}", align_bytes=64) for b in range(B)]
         q_scales = [keep.tile([P, NQ], U8, name=f"q_scales{b}", align_bytes=64) for b in range(B)]
 
         def quantize_queries(b):
             nc.vector.quantize_mx(out=q_codes[b][:].bitcast(FP8X4), scales=q_scales[b][:], in_=q_listed[b][:])
 
-        last_runs = placed.tile([P, 2, NQ], BF16, name="last_runs", align_bytes=64, offset=B * QUERY_BYTES)
-        for t in range(2, PACK):
-            gather(nc, False, q_words[0][:, :, t], q_raw[t], entries(query_list, 0, NQ))
-            gather(nc, False, last_runs[:, t - 2, :], q_raw[t], entries(query_list, NQ, NQ))
+        last_runs = placed.tile([P, 2, NQ], F32, name="last_runs", align_bytes=64, offset=B * QUERY_BYTES)
+        for h in range(2):
+            for b in range(B):
+                gather(nc, True, q_words[b][:, :, h], q_raw[h][:], entries(query_list, b * NQ, NQ))
+            gather(nc, False, q_words[0][:, :, 2 + h], q_raw[h][:, TQ:], entries(query_list, 0, NQ))
+            gather(nc, False, last_runs[:, h, :], q_raw[h][:, TQ:], entries(query_list, NQ, NQ))
         quantize_queries(0)
         nc.vector.tensor_copy(q_words[1][:, :, 2:4], last_runs[:].rearrange("p t c -> p c t"))
         quantize_keys(2)

@@ -100,7 +100,7 @@ def tile_attend_bothw_f_kernel(tc, qT, kT, kb, offq, offs, out):
         ]
         for i in range(2 * B):
             for t in range(2):
-                gather(nc, i > 0, late[i][:, t, :], k_raw[2 + t], entries(key_list, i * HALF, HALF))
+                gather(nc, 2 * i + t > 2, late[i][:, t, :], k_raw[2 + t], entries(key_list, i * HALF, HALF))
         halves = (by_half[0][:, 0], by_half[0][:, 1], by_half[1][:, 0], by_half[2][:, 0])
 
         def place_late(i):
@@ -110,7 +110,7 @@ def tile_attend_bothw_f_kernel(tc, qT, kT, kb, offq, offs, out):
         k_scales = [
             keep.tile([P, N], U8, name="k_scales0", align_bytes=64),
             keep.tile([P, HALF], U8, name="k_scales1", align_bytes=64),
-            placed.tile([P, HALF], U8, name="k_scales2", align_bytes=64, offset=0),
+            placed.tile([P, HALF], U8, name="k_scales2", align_bytes=64, offset=LATE_AT),
         ]
 
         def quantize_keys(i):
@@ -123,7 +123,7 @@ def tile_attend_bothw_f_kernel(tc, qT, kT, kb, offq, offs, out):
         place_late(3)
 
         q_listed = [
-            placed.tile([P, NQ * PACK], BF16, name=f"q_listed{b}", align_bytes=64, offset=b * QUERY_BYTES)
+            placed.tile([P, NQ * PACK], BF16, name=f"q_listed{b}", align_bytes=64, offset=LATE_AT + b * QUERY_BYTES)
             for b in range(B)
         ]
         q_words = [q_listed[b][:].rearrange("p (c t) -> p c t", t=PACK) for b in range(B)]

@@ -23,6 +23,7 @@ GROUP = 16
 HALF = N // 2
 PER = T // P
 BANK = 4
+DMA_ALIGN = 256
 QUERY_BYTES = 2 * NQ * PACK
 POOL_AT = 2 * N * PACK
 EARLY_AT = POOL_AT + 4 * T
@@ -58,7 +59,7 @@ def tile_attend_bothw_f_kernel(tc, qT, kT, kb, offq, offs, out):
         nc.sync.dma_start(key_list[:], offs)
         nc.sync.dma_start(query_list[:], offq)
         for u, at in enumerate((EARLY_AT, LATE_AT)):
-            raw = placed.tile([P, 2 * T], F32, name=f"k_raw{u}", align_bytes=64, offset=at)
+            raw = placed.tile([P, 2 * T], F32, name=f"k_raw{u}", align_bytes=DMA_ALIGN, offset=at)
             nc.scalar.dma_start(raw[:], k_rows[:, 2 * u * T : 2 * (u + 1) * T])
             k_raw.extend(raw[:, i * T : (i + 1) * T] for i in range(2))
 
@@ -87,7 +88,7 @@ def tile_attend_bothw_f_kernel(tc, qT, kT, kb, offq, offs, out):
             gather(nc, False, early[:, t * B * N : (t + 1) * B * N], k_raw[t], key_list[:])
         q_raw = []
         for h in range(2):
-            raw = placed.tile([P, 2 * TQ], F32, name=f"q_raw{h}", align_bytes=64, offset=EARLY_AT + 8 * h * TQ)
+            raw = placed.tile([P, 2 * TQ], F32, name=f"q_raw{h}", align_bytes=DMA_ALIGN, offset=EARLY_AT + 8 * h * TQ)
             nc.sync.dma_start(raw[:], q_rows[:, 2 * h * TQ : 2 * (h + 1) * TQ])
             q_raw.append(raw)
         low = early[:].rearrange("p (t i c) -> p i c t", t=2, c=HALF)
@@ -180,6 +181,6 @@ def tile_attend_bothw_f_kernel(tc, qT, kT, kb, offq, offs, out):
             inverse = keep.tile([P, 1], F32, name=f"inverse{b}")
             nc.vector.reciprocal(inverse[:], total[b][:])
             for i, cols in enumerate((slice(0, cut), slice(cut, N))):
-                y = keep.tile([P, cols.stop - cols.start], F32, name=f"y{b}_{i}")
+                y = keep.tile([P, cols.stop - cols.start], F32, name=f"y{b}_{i}", align_bytes=DMA_ALIGN)
                 nc.vector.tensor_scalar(y[:], e[b][:, cols], inverse[:], None, ALU.mult)
                 nc.sync.dma_start(out[b][:, cols], y[:])

@@ -134,12 +134,12 @@ def tile_attend_bothw_f_kernel(tc, qT, kT, kb, offq, offs, out):
         def quantize_queries(b):
             nc.vector.quantize_mx(out=q_codes[b][:].bitcast(FP8X4), scales=q_scales[b][:], in_=q_listed[b][:])
 
-        last_runs = placed.tile([P, 2, NQ], F32, name="last_runs", align_bytes=64, offset=B * QUERY_BYTES)
+        last_runs = placed.tile([P, 2, NQ], F32, name="last_runs", align_bytes=64, offset=LATE_AT + B * QUERY_BYTES)
         for h in range(2):
             for b in range(B):
                 gather(nc, True, q_words[b][:, :, h], q_raw[h][:], entries(query_list, b * NQ, NQ))
             gather(nc, False, q_words[0][:, :, 2 + h], q_raw[h][:, TQ:], entries(query_list, 0, NQ))
-            gather(nc, False, last_runs[:, h, :], q_raw[h][:, TQ:], entries(query_list, NQ, NQ))
+            gather(nc, h == 0, last_runs[:, h, :], q_raw[h][:, TQ:], entries(query_list, NQ, NQ))
         quantize_queries(0)
         nc.vector.tensor_copy(q_words[1][:, :, 2:4], last_runs[:].rearrange("p t c -> p c t"))
         quantize_keys(2)

@@ -87,9 +87,9 @@ def tile_attend_bothw_f_kernel(tc, qT, kT, kb, offq, offs, out):
         for t in range(2):
             gather(nc, False, early[:, t * B * N : (t + 1) * B * N], k_raw[t], key_list[:])
         q_raw = []
-        for h in range(2):
-            raw = placed.tile([P, 2 * TQ], F32, name=f"q_raw{h}", align_bytes=DMA_ALIGN, offset=EARLY_AT + 8 * h * TQ)
-            nc.sync.dma_start(raw[:], q_rows[:, 2 * h * TQ : 2 * (h + 1) * TQ])
+        for t0, n in ((0, 2), (2, 1), (3, 1)):
+            raw = placed.tile([P, n * TQ], F32, name=f"q_raw{t0}", align_bytes=DMA_ALIGN, offset=EARLY_AT + 4 * t0 * TQ)
+            nc.sync.dma_start(raw[:], q_rows[:, t0 * TQ : (t0 + n) * TQ])
             q_raw.append(raw)
         low = early[:].rearrange("p (t i c) -> p i c t", t=2, c=HALF)
         for i, (h0, n) in enumerate(parts):
@@ -135,11 +135,11 @@ def tile_attend_bothw_f_kernel(tc, qT, kT, kb, offq, offs, out):
             nc.vector.quantize_mx(out=q_codes[b][:].bitcast(FP8X4), scales=q_scales[b][:], in_=q_listed[b][:])
 
         last_runs = placed.tile([P, 2, NQ], F32, name="last_runs", align_bytes=64, offset=LATE_AT + B * QUERY_BYTES)
-        for h in range(2):
+        for h, second in enumerate((q_raw[0][:, TQ:], q_raw[2][:])):
             for b in range(B):
                 gather(nc, True, q_words[b][:, :, h], q_raw[h][:], entries(query_list, b * NQ, NQ))
-            gather(nc, False, q_words[0][:, :, 2 + h], q_raw[h][:, TQ:], entries(query_list, 0, NQ))
-            gather(nc, h == 0, last_runs[:, h, :], q_raw[h][:, TQ:], entries(query_list, NQ, NQ))
+            gather(nc, False, q_words[0][:, :, 2 + h], second, entries(query_list, 0, NQ))
+            gather(nc, h == 0, last_runs[:, h, :], second, entries(query_list, NQ, NQ))
         quantize_queries(0)
         nc.vector.tensor_copy(q_words[1][:, :, 2:4], last_runs[:].rearrange("p t c -> p c t"))
         quantize_keys(2)

@@ -48,9 +48,9 @@ def tile_attend_bothw_f_kernel(tc, qT, kT, kb, offq, offs, out):
         placed = ctx.enter_context(tc.tile_pool(name="placed", bufs=1))
         psum = ctx.enter_context(tc.psum_pool(name="psum", bufs=1))
 
-        key_list = keep.tile([P, B * N // GROUP], U16, name="key_list")
-        query_list = keep.tile([P, B * NQ // GROUP], U16, name="query_list")
-        bias_cols = keep.tile([P, PER], F32, name="bias_cols")
+        key_list = keep.tile([P, B * N // GROUP], U16, name="key_list", align_bytes=DMA_ALIGN)
+        query_list = keep.tile([P, B * NQ // GROUP], U16, name="query_list", align_bytes=DMA_ALIGN)
+        bias_cols = keep.tile([P, PER], F32, name="bias_cols", align_bytes=DMA_ALIGN)
         k_rows = kT.rearrange("(p t) c -> p (t c)", t=PACK)
         q_rows = qT.rearrange("(p t) c -> p (t c)", t=PACK)
         k_raw = []

from contextlib import ExitStack

import concourse.mybir as mybir
from concourse.masks import make_identity

B, N, T, D, NQ, TQ = 2, 512, 2048, 512, 128, 1024
FLOPS = 2 * B * NQ * N * D
BYTES = 4 * (D * TQ + D * T + T + B * NQ * N) + 2 * 128 * (16 + 64)

F32 = mybir.dt.float32
BF16 = mybir.dt.bfloat16
U32 = mybir.dt.uint32
U16 = mybir.dt.uint16
U8 = mybir.dt.uint8
FP8X4 = mybir.dt.float8_e4m3fn_x4
ALU = mybir.AluOpType
ACT = mybir.ActivationFunctionType
AX = mybir.AxisListType

P = 128
PACK = 4
GROUP = 16
HALF = N // 2
PER = T // P
BANK = 4
DMA_ALIGN = 256
QUERY_BYTES = 2 * NQ * PACK
POOL_AT = 2 * N * PACK
EARLY_AT = POOL_AT + 4 * T
LATE_AT = EARLY_AT + 4 * 2 * T


def entries(listed, first, count):
    return listed[:, first // GROUP : (first + count) // GROUP]


def gather(nc, on_scalar, out, window, listed):
    if on_scalar:
        nc.scalar.activation(out, window.indirect(listed), ACT.Copy)
    else:
        nc.vector.tensor_copy(out, window.indirect(listed))


def tile_attend_bothw_f_kernel(tc, qT, kT, kb, offq, offs, out):
    nc = tc.nc
    with ExitStack() as ctx:
        keep = ctx.enter_context(tc.tile_pool(name="keep", bufs=1))
        placed = ctx.enter_context(tc.tile_pool(name="placed", bufs=1))
        psum = ctx.enter_context(tc.psum_pool(name="psum", bufs=1))

        key_list = keep.tile([P, B * N // GROUP], U16, name="key_list", align_bytes=DMA_ALIGN)
        query_list = keep.tile([P, B * NQ // GROUP], U16, name="query_list", align_bytes=DMA_ALIGN)
        bias_cols = keep.tile([P, PER], F32, name="bias_cols", align_bytes=DMA_ALIGN)
        k_rows = kT.rearrange("(p t) c -> p (t c)", t=PACK)
        q_rows = qT.rearrange("(p t) c -> p (t c)", t=PACK)
        k_raw = []

        nc.sync.dma_start(bias_cols[:], kb[0:1, :].rearrange("o (p c) -> p (o c)", c=PER))
        nc.sync.dma_start(key_list[:], offs)
        nc.sync.dma_start(query_list[:], offq)
        for u, at in enumerate((EARLY_AT, LATE_AT)):
            raw = placed.tile([P, 2 * T], F32, name=f"k_raw{u}", align_bytes=DMA_ALIGN, offset=at)
            nc.scalar.dma_start(raw[:], k_rows[:, 2 * u * T : 2 * (u + 1) * T])
            k_raw.extend(raw[:, i * T : (i + 1) * T] for i in range(2))

        ident = keep.tile([P, P], F32, name="ident")
        make_identity(nc, ident[:])
        bias_pool = placed.tile([P, T], F32, name="bias_pool", align_bytes=64, offset=POOL_AT)
        in_order = bias_pool[:].rearrange("m (p j i) -> m j p i", j=PER // BANK, i=BANK)
        for j in range(PER // BANK):
            spread = psum.tile([P, BANK, P], F32, name=f"spread{j}")
            for i in range(BANK):
                c = j * BANK + i
                nc.tensor.transpose(spread[:, i, :], bias_cols[:, c : c + 1].to_broadcast([P, P]), ident[:])
            nc.scalar.activation(in_order[:, j], spread[:].rearrange("m i p -> m p i"), ACT.Copy)
        bias = keep.tile([P, B * N], F32, name="bias")
        gather(nc, True, bias[:], bias_pool[:], key_list[:])

        parts = ((0, 2), (2, 1), (3, 1))
        k_listed = [
            placed.tile([P, N * PACK], BF16, name="k_listed0", align_bytes=64, offset=0),
            keep.tile([P, HALF * PACK], BF16, name="k_listed1", align_bytes=64),
            keep.tile([P, HALF * PACK], BF16, name="k_listed2", align_bytes=64),
        ]
        by_half = [k[:].rearrange("p (i c w h) -> p i c w h", c=HALF, w=2, h=2) for k in k_listed]
        early = keep.tile([P, 2 * B * N], F32, name="early_runs")
        for t in range(2):
            gather(nc, False, early[:, t * B * N : (t + 1) * B * N], k_raw[t], key_list[:])
        q_raw = []
        for t0, n in ((0, 2), (2, 1), (3, 1)):
            raw = placed.tile([P, n * TQ], F32, name=f"q_raw{t0}", align_bytes=DMA_ALIGN, offset=EARLY_AT + 4 * t0 * TQ)
            nc.sync.dma_start(raw[:], q_rows[:, t0 * TQ : (t0 + n) * TQ])
            q_raw.append(raw)
        low = early[:].rearrange("p (t i c) -> p i c t", t=2, c=HALF)
        for i, (h0, n) in enumerate(parts):
            nc.vector.tensor_copy(by_half[i][:, :, :, :, 0], low[:, h0 : h0 + n])

        late = [
            placed.tile([P, 2, HALF], F32, name=f"late_runs{i}", align_bytes=64, offset=POOL_AT + i * 8 * HALF)
            for i in range(2 * B)
        ]
        for i in range(2 * B):
            for t in range(2):
                gather(nc, 2 * i + t > 2, late[i][:, t, :], k_raw[2 + t], entries(key_list, i * HALF, HALF))
        halves = (by_half[0][:, 0], by_half[0][:, 1], by_half[1][:, 0], by_half[2][:, 0])

        def place_late(i):
            nc.vector.tensor_copy(halves[i][:, :, :, 1], late[i][:].rearrange("p t c -> p c t"))

        k_codes = [keep.tile([P, n * HALF], U32, name=f"k_codes{h0}", align_bytes=64) for h0, n in parts]
        k_scales = [
            keep.tile([P, N], U8, name="k_scales0", align_bytes=64),
            keep.tile([P, HALF], U8, name="k_scales1", align_bytes=64),
            placed.tile([P, HALF], U8, name="k_scales2", align_bytes=64, offset=LATE_AT),
        ]

        def quantize_keys(i):
            nc.vector.quantize_mx(out=k_codes[i][:].bitcast(FP8X4), scales=k_scales[i][:], in_=k_listed[i][:])

        for i in range(3):
            place_late(i)
        quantize_keys(0)
        quantize_keys(1)
        place_late(3)

        q_listed = [
            placed.tile([P, NQ * PACK], BF16, name=f"q_listed{b}", align_bytes=64, offset=LATE_AT + b * QUERY_BYTES)
            for b in range(B)
        ]
        q_words = [q_listed[b][:].rearrange("p (c t) -> p c t", t=PACK) for b in range(B)]
        q_codes = [keep.tile([P, NQ], U32, name=f"q_codes{b}", align_bytes=64) for b in range(B)]
        q_scales = [keep.tile([P, NQ], U8, name=f"q_scales{b}", align_bytes=64) for b in range(B)]

        def quantize_queries(b):
            nc.vector.quantize_mx(out=q_codes[b][:].bitcast(FP8X4), scales=q_scales[b][:], in_=q_listed[b][:])

        last_runs = placed.tile([P, 2, NQ], F32, name="last_runs", align_bytes=64, offset=LATE_AT + B * QUERY_BYTES)
        for h, second in enumerate((q_raw[0][:, TQ:], q_raw[2][:])):
            for b in range(B):
                gather(nc, True, q_words[b][:, :, h], q_raw[h][:], entries(query_list, b * NQ, NQ))
            gather(nc, False, q_words[0][:, :, 2 + h], second, entries(query_list, 0, NQ))
            gather(nc, h == 0, last_runs[:, h, :], second, entries(query_list, NQ, NQ))
        quantize_queries(0)
        nc.vector.tensor_copy(q_words[1][:, :, 2:4], last_runs[:].rearrange("p t c -> p c t"))
        quantize_keys(2)
        quantize_queries(1)

        z = [keep.tile([P, N + 1 - b], F32, name=f"z{b}") for b in range(B)]
        neg_max = [keep.tile([P, 1], F32, name=f"neg_max{b}") for b in range(B)]

        def score(n, i, lo):
            b, c0 = n // 2, n % 2 * HALF
            acc = psum.tile([P, HALF], F32, name=f"scores{n}")
            nc.tensor.matmul_mx(
                out=acc[:],
                lhsT=q_codes[b][:].bitcast(FP8X4),
                lhsT_scale=q_scales[b][:],
                rhs=k_codes[i][:, lo : lo + HALF].bitcast(FP8X4),
                rhs_scale=k_scales[i][:, lo : lo + HALF],
                start=True,
                stop=True,
            )
            nc.vector.tensor_tensor(z[b][:, c0 : c0 + HALF], acc[:], bias[:, n * HALF : (n + 1) * HALF], ALU.add)

        score(0, 0, 0)
        score(1, 0, HALF)
        nc.vector.tensor_reduce(z[0][:, N:], z[0][:, :HALF], AX.X, ALU.max)
        score(2, 1, 0)
        score(3, 2, 0)
        nc.vector.tensor_reduce(neg_max[0][:], z[0][:, HALF:], AX.X, ALU.max, negate=True)
        nc.vector.tensor_reduce(neg_max[1][:], z[1][:], AX.X, ALU.max, negate=True)

        e = [keep.tile([P, N], F32, name=f"e{b}") for b in range(B)]
        total = [keep.tile([P, 1], F32, name=f"total{b}") for b in range(B)]
        for b in range(B):
            nc.scalar.activation(
                e[b][:], z[b][:, :N], ACT.Exp, bias=neg_max[b][:], scale=1.0, accum_out=total[b][:]
            )

        for b, cut in enumerate((N // 4, HALF)):
            inverse = keep.tile([P, 1], F32, name=f"inverse{b}")
            nc.vector.reciprocal(inverse[:], total[b][:])
            for i, cols in enumerate((slice(0, cut), slice(cut, N))):
                y = keep.tile([P, cols.stop - cols.start], F32, name=f"y{b}_{i}", align_bytes=DMA_ALIGN)
                nc.vector.tensor_scalar(y[:], e[b][:, cols], inverse[:], None, ALU.mult)
                nc.sync.dma_start(out[b][:, cols], y[:])
